import numpy as np
import ml_dtypes


def mxq(x, axis, fmt="e4m3"):
    dtype, down = {"e4m3": (ml_dtypes.float8_e4m3fn, 7), "e5m2": (ml_dtypes.float8_e5m2, 14)}[fmt]
    v = np.moveaxis(np.asarray(x, np.float32).astype(ml_dtypes.bfloat16).astype(np.float64), axis, -1)
    blocks = v.reshape(v.shape[:-1] + (-1, 32))
    amax = np.abs(blocks).max(-1, keepdims=True)
    byte = np.maximum(np.where(amax > 0, np.frexp(amax)[1] - 1 + 127, 0) - down, 1)
    scale = np.exp2(byte - 127.0)
    codes = (blocks / scale).astype(np.float32).astype(dtype).astype(np.float64)
    return np.moveaxis((codes * scale).reshape(v.shape), -1, axis)


WIDE = False


def mx_kscale(k):
    if not WIDE:
        return np.ones(k)
    levels = np.array([10, -10, 5, -5, 0])
    if k % 512:
        return np.exp2(np.random.permutation(np.resize(levels, k // 32))).repeat(32)
    a = np.empty((k // 512, 16))
    for p in range(k // 512):
        a[p, :8] = np.random.permutation(np.resize(levels, 8))
        for g in range(8):
            far = levels[np.abs(levels - a[p, g]) >= 10]
            a[p, g + 8] = far[np.random.randint(len(far))]
    return np.exp2(a.ravel()).repeat(32)


def f64(x):
    return np.asarray(x).astype(np.float64)


def striped(idx):
    return np.tile(idx.reshape(-1, 16).T, (8, 1)).astype(np.uint16)


def unstriped(offs):
    return offs[:16].T.reshape(-1).astype(np.int64)


def pack_weight(w):
    k, n = w.shape
    w = f64(np.asarray(w, np.float32).astype(ml_dtypes.bfloat16)).reshape(k // 32, 32, n)
    amax = np.abs(w).max(1)
    byte = np.clip(np.where(amax > 0, np.frexp(amax)[1] - 1 + 127 - 7, 1), 1, 254)
    scaled = (w * np.exp2(127.0 - byte)[:, None, :]).reshape(k, n).astype(np.float32)
    words = np.ascontiguousarray(scaled.reshape(k // 512, 128, 4, n).transpose(0, 1, 3, 2)).astype(ml_dtypes.float8_e4m3fn).view(np.uint8)
    return words, np.ascontiguousarray(byte.astype(np.uint8).reshape(k // 512, 16, n))


def unpack_weight(words, scales):
    g, p, n, _ = words.shape
    vals = np.ascontiguousarray(words).view(ml_dtypes.float8_e4m3fn).astype(np.float64) * np.repeat(np.exp2(scales.astype(np.float64) - 127.0), 8, axis=1)[..., None]
    return vals.transpose(0, 1, 3, 2).reshape(g * 512, n)


def relu(v):
    return np.maximum(v, 0.0)


K, T, S, H, N, R = 512, 2048, 512, 512, 128, 256
P = 2 ** 7


def setup_inputs():
    n = np.random.standard_normal
    s = mx_kscale(K)[:, None]
    u = mx_kscale(H)
    packed_xT = pack_weight(n((K, T)) * s)
    return {
        "x_words": packed_xT[0],
        "x_scales": packed_xT[1],
        "w1": (n((K, H)) / np.sqrt(K) / s * u).astype(np.float32),
        "w2": (n((H, N)) / np.sqrt(H) / u[:, None]).astype(np.float32),
        "temb": (n((H, R)) * u[:, None]).astype(np.float32),
        "lat": (n((N, S))).astype(np.float32),
        "csig": (np.tile(np.random.uniform(1.0, 1.2, R), (P, 1))).astype(np.float32),
        "cnoise": (np.tile(np.random.uniform(0.1, 0.8, R), (P, 1))).astype(np.float32),
        "offs": striped(np.random.permutation(T)[:S]),
        "step": striped(np.random.permutation(np.concatenate([np.arange(R), np.random.randint(0, R, S - R)]))),
    }


def reference(x_words, x_scales, w1, w2, temb, lat, csig, cnoise, offs, step):
    xq = unpack_weight(x_words, x_scales)[:, unstriped(offs)]
    h = relu((mxq(f64(w1), 0, "e4m3").T @ xq) + f64(temb)[:, unstriped(step)])
    ee = mxq(f64(w2), 0, "e4m3").T @ mxq(h, 0, "e4m3")
    return f64(lat) * (f64(csig)[:1][:, unstriped(step)]) - (ee * (f64(cnoise)[:1][:, unstriped(step)]))

@@ -1,0 +1,187 @@
+from contextlib import ExitStack
+
+import concourse.mybir as mybir
+from concourse.masks import make_identity
+
+K, T, S, H, N, R = 512, 2048, 512, 512, 128, 256
+FLOPS = 2 * K * H * S + 2 * H * N * S
+
+F32 = mybir.dt.float32
+BF16 = mybir.dt.bfloat16
+I32 = mybir.dt.int32
+U32 = mybir.dt.uint32
+U16 = mybir.dt.uint16
+U8 = mybir.dt.uint8
+FP8X4 = mybir.dt.float8_e4m3fn_x4
+ADD = mybir.AluOpType.add
+COPY = mybir.ActivationFunctionType.Copy
+RELU = mybir.ActivationFunctionType.Relu
+
+P = 128
+PACK = 4
+CHUNK = 128
+CHUNKS = S // CHUNK
+HALF = S // 2
+WINDOW = 3 * R
+LANES = 16
+
+
+def tile_picked_yddpm_relu_p_kernel(tc, x_words, x_scales, w1, w2, temb, lat, csig, cnoise, offs, step, out):
+    nc = tc.nc
+    with ExitStack() as ctx:
+        held = ctx.enter_context(tc.tile_pool(name="held", bufs=1))
+        psum_h = ctx.enter_context(tc.psum_pool(name="psum_h", bufs=CHUNKS))
+        psum_mid = ctx.enter_context(tc.psum_pool(name="psum_mid", bufs=2))
+        psum_out = ctx.enter_context(tc.psum_pool(name="psum_out", bufs=2))
+
+        step_list = held.tile([P, S // LANES], U16, name="step_list")
+        offs_list = held.tile([P, S // LANES], U16, name="offs_list")
+        coef = held.tile([P, WINDOW], F32, name="coef")
+        emb = held.tile([P, (PACK - 2) * R + WINDOW], F32, name="emb")
+        emb_last = held.tile([P, WINDOW], F32, name="emb_last")
+        scale_table = held.tile([P, T], U8, name="scale_table")
+        word_table = held.tile([P, T], I32, name="word_table")
+        w1_raw = held.tile([P, PACK, H], F32, name="w1_raw")
+        w2_raw = held.tile([P, PACK, N], F32, name="w2_raw")
+        lat_sb = held.tile([P, S], F32, name="lat_sb")
+        ident = held.tile([P, P], F32, name="ident")
+
+        nc.vector.memset(scale_table[:].bitcast(I32), 0)
+        nc.vector.memset(coef[:, R:], 0.0)
+        nc.vector.memset(emb[:, (PACK - 1) * R :], 0.0)
+        nc.vector.memset(emb_last[:, R:], 0.0)
+        make_identity(nc, ident[:])
+
+        nc.sync.dma_start(step_list[:], step)
+        nc.sync.dma_start(coef[: P // 2, :R], csig[: P // 2, :])
+        nc.sync.dma_start(coef[P // 2 :, :R], cnoise[P // 2 :, :])
+        temb_rows = temb.rearrange("(p t) r -> p (t r)", t=PACK)
+        nc.sync.dma_start(emb[:, : (PACK - 1) * R], temb_rows[:, : (PACK - 1) * R])
+        nc.sync.dma_start(offs_list[:], offs)
+        nc.sync.dma_start(w1_raw[:], w1.rearrange("(p j) c -> p j c", j=PACK))
+        nc.sync.dma_start(word_table[:], x_words[0].rearrange("p n t -> p (n t)").bitcast(I32))
+        nc.sync.dma_start(emb_last[:, :R], temb_rows[:, (PACK - 1) * R :])
+        nc.sync.dma_start(w2_raw[:], w2.rearrange("(p j) m -> p j m", j=PACK))
+        nc.sync.dma_start(lat_sb[:], lat)
+        for q in range(4):
+            nc.scalar.dma_start(
+                scale_table[32 * q : 32 * q + 4, :].bitcast(I32),
+                x_scales[0, 4 * q : 4 * q + 4, :].bitcast(I32),
+            )
+
+        coef_g = held.tile([P, S], F32, name="coef_g")
+        nc.vector.tensor_copy(coef_g[:], coef[:].indirect(step_list[:]))
+        emb_g = held.tile([P, PACK, S], F32, name="emb_g")
+        for t in range(PACK - 1):
+            nc.vector.tensor_copy(emb_g[:, t, :], emb[:, t * R : t * R + WINDOW].indirect(step_list[:]))
+        x_sc = held.tile([P, S], U8, name="x_sc", align_bytes=64)
+        nc.vector.tensor_copy(x_sc[:], scale_table[:].indirect(offs_list[:]))
+
+        w1_bf = held.tile([P, PACK, P, PACK], BF16, name="w1_bf", align_bytes=64)
+        nc.scalar.copy(
+            w1_bf[:].rearrange("p t m j -> p m j t"),
+            w1_raw[:].rearrange("p j (m t) -> p m j t", t=PACK),
+        )
+        w1_codes = held.tile([P, H], U32, name="w1_codes", align_bytes=64)
+        w1_sc = held.tile([P, H], U8, name="w1_sc", align_bytes=64)
+        nc.vector.quantize_mx(
+            out=w1_codes[:].bitcast(FP8X4), scales=w1_sc[:], in_=w1_bf[:].rearrange("p t m j -> p (t m j)")
+        )
+
+        x_codes = held.tile([P, S], U32, name="x_codes", align_bytes=64)
+        for half in range(2):
+            entries = slice(half * HALF // LANES, (half + 1) * HALF // LANES)
+            nc.vector.tensor_copy(
+                x_codes[:, half * HALF : (half + 1) * HALF],
+                word_table[:].bitcast(U32).indirect(offs_list[:, entries]),
+            )
+        nc.vector.tensor_copy(emb_g[:, PACK - 1, :], emb_last[:].indirect(step_list[:]))
+
+        coef_t = psum_mid.tile([P, CHUNKS, P], F32, name="coef_t", tag="mid")
+        for c in range(CHUNKS):
+            nc.tensor.transpose(coef_t[:, c, :], coef_g[:, c * CHUNK : (c + 1) * CHUNK], ident[:])
+        sig_col = held.tile([P, CHUNKS], F32, name="sig_col")
+        neg_noise_col = held.tile([P, CHUNKS], F32, name="neg_noise_col")
+        nc.scalar.copy(sig_col[:], coef_t[:, :, 0])
+        nc.scalar.activation(neg_noise_col[:], coef_t[:, :, P // 2], COPY, scale=-1.0)
+
+        w2_bf = held.tile([P, N, PACK], BF16, name="w2_bf", align_bytes=64)
+        nc.scalar.copy(
+            w2_bf[:].rearrange("p (a i) j -> p a j i", i=4),
+            w2_raw[:].rearrange("p j (a i) -> p a j i", i=4),
+        )
+        w2_codes = held.tile([P, N], U32, name="w2_codes", align_bytes=64)
+        w2_sc = held.tile([P, N], U8, name="w2_sc", align_bytes=64)
+        nc.vector.quantize_mx(
+            out=w2_codes[:].bitcast(FP8X4), scales=w2_sc[:], in_=w2_bf[:].rearrange("p m j -> p (m j)")
+        )
+
+        lat_t = psum_mid.tile([P, CHUNKS, P], F32, name="lat_t", tag="mid")
+        kept = held.tile([P, CHUNKS, N], F32, name="kept")
+        for c in range(CHUNKS):
+            nc.tensor.transpose(lat_t[:, c, :], lat_sb[:, c * CHUNK : (c + 1) * CHUNK], ident[:])
+        for c in range(CHUNKS):
+            nc.scalar.activation(kept[:, c, :], lat_t[:, c, :], COPY, scale=sig_col[:, c : c + 1])
+
+        pre = held.tile([P, CHUNKS, PACK, CHUNK], F32, name="pre")
+        h_bf = held.tile([P, CHUNKS, CHUNK, PACK], BF16, name="h_bf", align_bytes=64)
+        h_codes = held.tile([P, S], U32, name="h_codes", align_bytes=64)
+        h_sc = held.tile([P, S], U8, name="h_sc", align_bytes=64)
+        removed = held.tile([P, CHUNKS, N], F32, name="removed")
+        result = held.tile([P, S], F32, name="result")
+
+        def first_layer(c):
+            cols = slice(c * CHUNK, (c + 1) * CHUNK)
+            acc = psum_h.tile([P, PACK, CHUNK], F32, name="acc")
+            for t in range(PACK):
+                chans = slice(t * P, (t + 1) * P)
+                nc.tensor.matmul_mx(
+                    out=acc[:, t, :],
+                    lhsT=w1_codes[:, chans].bitcast(FP8X4),
+                    lhsT_scale=w1_sc[:, chans],
+                    rhs=x_codes[:, cols].bitcast(FP8X4),
+                    rhs_scale=x_sc[:, cols],
+                    start=True,
+                    stop=True,
+                )
+            nc.vector.tensor_tensor(pre[:, c], acc[:], emb_g[:, :, cols], ADD)
+            nc.scalar.activation(
+                h_bf[:, c].rearrange("p (a i) t -> p a t i", i=4),
+                pre[:, c].rearrange("p t (a i) -> p a t i", i=4),
+                RELU,
+            )
+
+        def second_layer(c):
+            cols = slice(c * CHUNK, (c + 1) * CHUNK)
+            nc.vector.quantize_mx(
+                out=h_codes[:, cols].bitcast(FP8X4),
+                scales=h_sc[:, cols],
+                in_=h_bf[:, c].rearrange("p n t -> p (n t)"),
+            )
+            noise_t = psum_mid.tile([P, N], F32, name="noise_t", tag="mid")
+            nc.tensor.matmul_mx(
+                out=noise_t[:],
+                lhsT=h_codes[:, cols].bitcast(FP8X4),
+                lhsT_scale=h_sc[:, cols],
+                rhs=w2_codes[:].bitcast(FP8X4),
+                rhs_scale=w2_sc[:],
+                start=True,
+                stop=True,
+            )
+            nc.scalar.activation(removed[:, c, :], noise_t[:], COPY, scale=neg_noise_col[:, c : c + 1])
+
+        def way_out(c):
+            cols = slice(c * CHUNK, (c + 1) * CHUNK)
+            total = psum_out.tile([P, CHUNK], F32, name="total")
+            nc.tensor.matmul(total[:], kept[:, c, :], ident[:], start=True, stop=False, is_transpose=True)
+            nc.tensor.matmul(total[:], removed[:, c, :], ident[:], start=False, stop=True, is_transpose=True)
+            nc.vector.tensor_copy(result[:, cols], total[:])
+            nc.sync.dma_start(out[:, cols], result[:, cols])
+
+        for c in range(CHUNKS + 1):
+            if c < CHUNKS:
+                first_layer(c)
+            if c >= 1:
+                second_layer(c - 1)
+        for c in range(CHUNKS):
+            way_out(c)

@@ -14,6 +14,8 @@ U16 = mybir.dt.uint16
 U8 = mybir.dt.uint8
 FP8X4 = mybir.dt.float8_e4m3fn_x4
 ADD = mybir.AluOpType.add
+MULT = mybir.AluOpType.mult
+SUBTRACT = mybir.AluOpType.subtract
 COPY = mybir.ActivationFunctionType.Copy
 RELU = mybir.ActivationFunctionType.Relu
 
@@ -22,7 +24,8 @@ PACK = 4
 CHUNK = 128
 CHUNKS = S // CHUNK
 HALF = S // 2
-WINDOW = 3 * R
+LAST = CHUNKS - 1
+WINDOW = 704
 LANES = 16
 
 
@@ -31,8 +34,7 @@ def tile_picked_yddpm_relu_p_kernel(tc, x_words, x_scales, w1, w2, temb, lat, cs
     with ExitStack() as ctx:
         held = ctx.enter_context(tc.tile_pool(name="held", bufs=1))
         psum_h = ctx.enter_context(tc.psum_pool(name="psum_h", bufs=CHUNKS))
-        psum_mid = ctx.enter_context(tc.psum_pool(name="psum_mid", bufs=2))
-        psum_out = ctx.enter_context(tc.psum_pool(name="psum_out", bufs=2))
+        psum_mid = ctx.enter_context(tc.psum_pool(name="psum_mid", bufs=4))
 
         step_list = held.tile([P, S // LANES], U16, name="step_list")
         offs_list = held.tile([P, S // LANES], U16, name="offs_list")
@@ -41,15 +43,15 @@ def tile_picked_yddpm_relu_p_kernel(tc, x_words, x_scales, w1, w2, temb, lat, cs
         emb_last = held.tile([P, WINDOW], F32, name="emb_last")
         scale_table = held.tile([P, T], U8, name="scale_table")
         word_table = held.tile([P, T], I32, name="word_table")
-        w1_raw = held.tile([P, PACK, H], F32, name="w1_raw")
+        w1_raw = [held.tile([P, PACK, H // 2], F32, name="w1_raw%d" % u) for u in range(2)]
         w2_raw = held.tile([P, PACK, N], F32, name="w2_raw")
         lat_sb = held.tile([P, S], F32, name="lat_sb")
         ident = held.tile([P, P], F32, name="ident")
 
         nc.vector.memset(scale_table[:].bitcast(I32), 0)
         nc.vector.memset(coef[:, R:], 0.0)
-        nc.vector.memset(emb[:, (PACK - 1) * R :], 0.0)
-        nc.vector.memset(emb_last[:, R:], 0.0)
+        nc.gpsimd.memset(emb[:, (PACK - 1) * R :], 0.0)
+        nc.gpsimd.memset(emb_last[:, R:], 0.0)
         make_identity(nc, ident[:])
 
         nc.sync.dma_start(step_list[:], step)
@@ -58,7 +60,9 @@ def tile_picked_yddpm_relu_p_kernel(tc, x_words, x_scales, w1, w2, temb, lat, cs
         temb_rows = temb.rearrange("(p t) r -> p (t r)", t=PACK)
         nc.sync.dma_start(emb[:, : (PACK - 1) * R], temb_rows[:, : (PACK - 1) * R])
         nc.sync.dma_start(offs_list[:], offs)
-        nc.sync.dma_start(w1_raw[:], w1.rearrange("(p j) c -> p j c", j=PACK))
+        w1_rows = w1.rearrange("(p j) c -> p j c", j=PACK)
+        for u in range(2):
+            nc.sync.dma_start(w1_raw[u][:], w1_rows[:, :, u * H // 2 : (u + 1) * H // 2])
         nc.sync.dma_start(word_table[:], x_words[0].rearrange("p n t -> p (n t)").bitcast(I32))
         nc.sync.dma_start(emb_last[:, :R], temb_rows[:, (PACK - 1) * R :])
         nc.sync.dma_start(w2_raw[:], w2.rearrange("(p j) m -> p j m", j=PACK))
@@ -71,39 +75,43 @@ def tile_picked_yddpm_relu_p_kernel(tc, x_words, x_scales, w1, w2, temb, lat, cs
 
         coef_g = held.tile([P, S], F32, name="coef_g")
         nc.vector.tensor_copy(coef_g[:], coef[:].indirect(step_list[:]))
-        emb_g = held.tile([P, PACK, S], F32, name="emb_g")
+        staging = held.tile([P, (PACK + 1) * S], F32, name="staging", align_bytes=64)
+        emb_g = staging[:, : PACK * S].rearrange("p (t s) -> p t s", t=PACK)
+        w1_bf = staging[:, (PACK - 1) * S :].bitcast(BF16)
         for t in range(PACK - 1):
             nc.vector.tensor_copy(emb_g[:, t, :], emb[:, t * R : t * R + WINDOW].indirect(step_list[:]))
         x_sc = held.tile([P, S], U8, name="x_sc", align_bytes=64)
         nc.vector.tensor_copy(x_sc[:], scale_table[:].indirect(offs_list[:]))
 
-        w1_bf = held.tile([P, PACK, P, PACK], BF16, name="w1_bf", align_bytes=64)
-        nc.scalar.copy(
-            w1_bf[:].rearrange("p t m j -> p m j t"),
-            w1_raw[:].rearrange("p j (m t) -> p m j t", t=PACK),
-        )
+        for u in range(2):
+            nc.scalar.copy(
+                w1_bf.rearrange("p (t m j) -> p m j t", t=PACK, j=PACK)[:, u * P // 2 : (u + 1) * P // 2],
+                w1_raw[u][:].rearrange("p j (m t) -> p m j t", t=PACK),
+            )
         w1_codes = held.tile([P, H], U32, name="w1_codes", align_bytes=64)
         w1_sc = held.tile([P, H], U8, name="w1_sc", align_bytes=64)
         nc.vector.quantize_mx(
-            out=w1_codes[:].bitcast(FP8X4), scales=w1_sc[:], in_=w1_bf[:].rearrange("p t m j -> p (t m j)")
+            out=w1_codes[:].bitcast(FP8X4), scales=w1_sc[:], in_=w1_bf
         )
 
         x_codes = held.tile([P, S], U32, name="x_codes", align_bytes=64)
-        for half in range(2):
-            entries = slice(half * HALF // LANES, (half + 1) * HALF // LANES)
-            nc.vector.tensor_copy(
-                x_codes[:, half * HALF : (half + 1) * HALF],
-                word_table[:].bitcast(U32).indirect(offs_list[:, entries]),
-            )
+        nc.vector.tensor_copy(x_codes[:], word_table[:].bitcast(U32).indirect(offs_list[:]))
         nc.vector.tensor_copy(emb_g[:, PACK - 1, :], emb_last[:].indirect(step_list[:]))
 
         coef_t = psum_mid.tile([P, CHUNKS, P], F32, name="coef_t", tag="mid")
         for c in range(CHUNKS):
             nc.tensor.transpose(coef_t[:, c, :], coef_g[:, c * CHUNK : (c + 1) * CHUNK], ident[:])
-        sig_col = held.tile([P, CHUNKS], F32, name="sig_col")
-        neg_noise_col = held.tile([P, CHUNKS], F32, name="neg_noise_col")
-        nc.scalar.copy(sig_col[:], coef_t[:, :, 0])
-        nc.scalar.activation(neg_noise_col[:], coef_t[:, :, P // 2], COPY, scale=-1.0)
+        coef_col = held.tile([P, CHUNKS, 2], F32, name="coef_col")
+        nc.scalar.copy(coef_col[:], coef_t[:, :, 0 : P : P // 2])
+        neg_noise_col = held.tile([P, 2], F32, name="neg_noise_col")
+        nc.scalar.activation(neg_noise_col[:], coef_t[:, :2, P // 2], COPY, scale=-1.0)
+        noise_ps = psum_mid.tile([P, HALF], F32, name="noise_ps", tag="mid")
+        for c in range(2):
+            nc.tensor.transpose(
+                noise_ps[:, c * CHUNK : (c + 1) * CHUNK], coef_col[:, 2 + c, 1:2].to_broadcast([P, P]), ident[:]
+            )
+        noise_factor = held.tile([P, HALF], F32, name="noise_factor")
+        nc.scalar.copy(noise_factor[:], noise_ps[:])
 
         w2_bf = held.tile([P, N, PACK], BF16, name="w2_bf", align_bytes=64)
         nc.scalar.copy(
@@ -117,22 +125,26 @@ def tile_picked_yddpm_relu_p_kernel(tc, x_words, x_scales, w1, w2, temb, lat, cs
         )
 
         lat_t = psum_mid.tile([P, CHUNKS, P], F32, name="lat_t", tag="mid")
-        kept = held.tile([P, CHUNKS, N], F32, name="kept")
+        kept_t = held.tile([P, CHUNKS, N], F32, name="kept_t")
+        kept = psum_mid.tile([P, HALF], F32, name="kept", tag="mid")
         for c in range(CHUNKS):
             nc.tensor.transpose(lat_t[:, c, :], lat_sb[:, c * CHUNK : (c + 1) * CHUNK], ident[:])
         for c in range(CHUNKS):
-            nc.scalar.activation(kept[:, c, :], lat_t[:, c, :], COPY, scale=sig_col[:, c : c + 1])
+            nc.scalar.activation(kept_t[:, c, :], lat_t[:, c, :], COPY, scale=coef_col[:, c, 0:1])
+        for c in range(2):
+            nc.tensor.transpose(kept[:, c * CHUNK : (c + 1) * CHUNK], kept_t[:, 2 + c, :], ident[:])
 
         pre = held.tile([P, CHUNKS, PACK, CHUNK], F32, name="pre")
-        h_bf = held.tile([P, CHUNKS, CHUNK, PACK], BF16, name="h_bf", align_bytes=64)
+        h_bf = held.tile([P, CHUNKS, PACK * CHUNK], BF16, name="h_bf", align_bytes=64)
         h_codes = held.tile([P, S], U32, name="h_codes", align_bytes=64)
         h_sc = held.tile([P, S], U8, name="h_sc", align_bytes=64)
-        removed = held.tile([P, CHUNKS, N], F32, name="removed")
+        removed_t = held.tile([P, 2, N], F32, name="removed_t")
+        removed = held.tile([P, HALF], F32, name="removed")
         result = held.tile([P, S], F32, name="result")
 
-        def first_layer(c):
+        def first_product(c):
             cols = slice(c * CHUNK, (c + 1) * CHUNK)
-            acc = psum_h.tile([P, PACK, CHUNK], F32, name="acc")
+            acc = psum_h.tile([P, PACK, CHUNK], F32, name="acc", tag="wide")
             for t in range(PACK):
                 chans = slice(t * P, (t + 1) * P)
                 nc.tensor.matmul_mx(
@@ -144,44 +156,60 @@ def tile_picked_yddpm_relu_p_kernel(tc, x_words, x_scales, w1, w2, temb, lat, cs
                     start=True,
                     stop=True,
                 )
-            nc.vector.tensor_tensor(pre[:, c], acc[:], emb_g[:, :, cols], ADD)
-            nc.scalar.activation(
-                h_bf[:, c].rearrange("p (a i) t -> p a t i", i=4),
-                pre[:, c].rearrange("p t (a i) -> p a t i", i=4),
-                RELU,
+            return acc
+
+        def relu_views(c, first=0, count=CHUNK):
+            return (
+                h_bf[:, c, PACK * first : PACK * (first + count)].rearrange("p (a i t) -> p a t i", i=4, t=PACK),
+                pre[:, c, :, first : first + count].rearrange("p t (a i) -> p a t i", i=4),
             )
 
-        def second_layer(c):
-            cols = slice(c * CHUNK, (c + 1) * CHUNK)
+        def quantise_hidden(c, count=1):
+            cols = slice(c * CHUNK, (c + count) * CHUNK)
             nc.vector.quantize_mx(
                 out=h_codes[:, cols].bitcast(FP8X4),
                 scales=h_sc[:, cols],
-                in_=h_bf[:, c].rearrange("p n t -> p (n t)"),
+                in_=h_bf[:, c : c + count, :].rearrange("p c w -> p (c w)"),
             )
-            noise_t = psum_mid.tile([P, N], F32, name="noise_t", tag="mid")
-            nc.tensor.matmul_mx(
-                out=noise_t[:],
-                lhsT=h_codes[:, cols].bitcast(FP8X4),
-                lhsT_scale=h_sc[:, cols],
-                rhs=w2_codes[:].bitcast(FP8X4),
-                rhs_scale=w2_sc[:],
-                start=True,
-                stop=True,
-            )
-            nc.scalar.activation(removed[:, c, :], noise_t[:], COPY, scale=neg_noise_col[:, c : c + 1])
 
-        def way_out(c):
+        def second_product(dst, c, tokens_on_partitions):
             cols = slice(c * CHUNK, (c + 1) * CHUNK)
-            total = psum_out.tile([P, CHUNK], F32, name="total")
-            nc.tensor.matmul(total[:], kept[:, c, :], ident[:], start=True, stop=False, is_transpose=True)
-            nc.tensor.matmul(total[:], removed[:, c, :], ident[:], start=False, stop=True, is_transpose=True)
-            nc.vector.tensor_copy(result[:, cols], total[:])
-            nc.sync.dma_start(out[:, cols], result[:, cols])
+            hidden = (h_codes[:, cols].bitcast(FP8X4), h_sc[:, cols])
+            weights = (w2_codes[:].bitcast(FP8X4), w2_sc[:])
+            still, moving = (hidden, weights) if tokens_on_partitions else (weights, hidden)
+            nc.tensor.matmul_mx(
+                out=dst, lhsT=still[0], lhsT_scale=still[1], rhs=moving[0], rhs_scale=moving[1], start=True, stop=True
+            )
 
-        for c in range(CHUNKS + 1):
-            if c < CHUNKS:
-                first_layer(c)
-            if c >= 1:
-                second_layer(c - 1)
+        accs = [first_product(c) for c in range(CHUNKS)]
         for c in range(CHUNKS):
-            way_out(c)
+            nc.vector.tensor_tensor(pre[:, c], accs[c][:], emb_g[:, :, c * CHUNK : (c + 1) * CHUNK], ADD)
+            if c < LAST:
+                nc.scalar.activation(*relu_views(c), RELU)
+            if c >= 2:
+                quantise_hidden(c - 2)
+        nc.scalar.activation(*relu_views(LAST, 0, CHUNK // 2), RELU)
+        nc.vector.tensor_scalar_max(*relu_views(LAST, CHUNK // 2, CHUNK // 2), 0.0)
+        quantise_hidden(2)
+        quantise_hidden(LAST)
+
+        totals = [psum_h.tile([P, CHUNK], F32, name="total%d" % c, tag="wide") for c in range(2)]
+        for c in range(2):
+            noise_t = psum_h.tile([P, N], F32, name="noise_t", tag="wide")
+            second_product(noise_t[:], c, True)
+            nc.scalar.activation(removed_t[:, c, :], noise_t[:], COPY, scale=neg_noise_col[:, c : c + 1])
+        for c in range(2):
+            cols = slice(c * CHUNK, (c + 1) * CHUNK)
+            noise = psum_mid.tile([P, CHUNK], F32, name="noise", tag="mid")
+            second_product(noise[:], 2 + c, False)
+            nc.vector.tensor_tensor(removed[:, cols], noise[:], noise_factor[:, cols], MULT)
+        for c in range(2):
+            cols = slice(c * CHUNK, (c + 1) * CHUNK)
+            nc.vector.tensor_tensor(result[:, HALF:][:, cols], kept[:, cols], removed[:, cols], SUBTRACT)
+        for c in range(2):
+            nc.tensor.matmul(totals[c][:], kept_t[:, c, :], ident[:], start=True, stop=False, is_transpose=True)
+            nc.tensor.matmul(totals[c][:], removed_t[:, c, :], ident[:], start=False, stop=True, is_transpose=True)
+            nc.scalar.copy(result[:, c * CHUNK : (c + 1) * CHUNK], totals[c][:])
+        nc.sync.dma_start(out[:, :HALF], result[:, :HALF])
+        for c in range(2, CHUNKS):
+            nc.sync.dma_start(out[:, c * CHUNK : (c + 1) * CHUNK], result[:, c * CHUNK : (c + 1) * CHUNK])

@@ -48,10 +48,10 @@ def tile_picked_yddpm_relu_p_kernel(tc, x_words, x_scales, w1, w2, temb, lat, cs
         lat_sb = held.tile([P, S], F32, name="lat_sb")
         ident = held.tile([P, P], F32, name="ident")
 
-        nc.vector.memset(scale_table[:].bitcast(I32), 0)
+        nc.gpsimd.memset(scale_table[:].bitcast(I32), 0)
         nc.vector.memset(coef[:, R:], 0.0)
-        nc.gpsimd.memset(emb[:, (PACK - 1) * R :], 0.0)
-        nc.gpsimd.memset(emb_last[:, R:], 0.0)
+        nc.vector.memset(emb[:, (PACK - 1) * R :], 0.0)
+        nc.vector.memset(emb_last[:, R:], 0.0)
         make_identity(nc, ident[:])
 
         nc.sync.dma_start(step_list[:], step)
@@ -59,19 +59,19 @@ def tile_picked_yddpm_relu_p_kernel(tc, x_words, x_scales, w1, w2, temb, lat, cs
         nc.sync.dma_start(coef[P // 2 :, :R], cnoise[P // 2 :, :])
         temb_rows = temb.rearrange("(p t) r -> p (t r)", t=PACK)
         nc.sync.dma_start(emb[:, : (PACK - 1) * R], temb_rows[:, : (PACK - 1) * R])
-        nc.sync.dma_start(offs_list[:], offs)
         w1_rows = w1.rearrange("(p j) c -> p j c", j=PACK)
         for u in range(2):
             nc.sync.dma_start(w1_raw[u][:], w1_rows[:, :, u * H // 2 : (u + 1) * H // 2])
-        nc.sync.dma_start(word_table[:], x_words[0].rearrange("p n t -> p (n t)").bitcast(I32))
-        nc.sync.dma_start(emb_last[:, :R], temb_rows[:, (PACK - 1) * R :])
-        nc.sync.dma_start(w2_raw[:], w2.rearrange("(p j) m -> p j m", j=PACK))
-        nc.sync.dma_start(lat_sb[:], lat)
         for q in range(4):
-            nc.scalar.dma_start(
+            nc.sync.dma_start(
                 scale_table[32 * q : 32 * q + 4, :].bitcast(I32),
                 x_scales[0, 4 * q : 4 * q + 4, :].bitcast(I32),
             )
+        nc.sync.dma_start(offs_list[:], offs)
+        nc.sync.dma_start(word_table[:], x_words[0].rearrange("p n t -> p (n t)").bitcast(I32))
+        nc.sync.dma_start(lat_sb[:], lat)
+        nc.sync.dma_start(emb_last[:, :R], temb_rows[:, (PACK - 1) * R :])
+        nc.sync.dma_start(w2_raw[:], w2.rearrange("(p j) m -> p j m", j=PACK))
 
         coef_g = held.tile([P, S], F32, name="coef_g")
         nc.vector.tensor_copy(coef_g[:], coef[:].indirect(step_list[:]))
@@ -95,7 +95,12 @@ def tile_picked_yddpm_relu_p_kernel(tc, x_words, x_scales, w1, w2, temb, lat, cs
         )
 
         x_codes = held.tile([P, S], U32, name="x_codes", align_bytes=64)
-        nc.vector.tensor_copy(x_codes[:], word_table[:].bitcast(U32).indirect(offs_list[:]))
+        for half in range(2):
+            entries = slice(half * HALF // LANES, (half + 1) * HALF // LANES)
+            nc.vector.tensor_copy(
+                x_codes[:, half * HALF : (half + 1) * HALF],
+                word_table[:].bitcast(U32).indirect(offs_list[:, entries]),
+            )
         nc.vector.tensor_copy(emb_g[:, PACK - 1, :], emb_last[:].indirect(step_list[:]))
 
         coef_t = psum_mid.tile([P, CHUNKS, P], F32, name="coef_t", tag="mid")
@@ -126,13 +131,10 @@ def tile_picked_yddpm_relu_p_kernel(tc, x_words, x_scales, w1, w2, temb, lat, cs
 
         lat_t = psum_mid.tile([P, CHUNKS, P], F32, name="lat_t", tag="mid")
         kept_t = held.tile([P, CHUNKS, N], F32, name="kept_t")
-        kept = psum_mid.tile([P, HALF], F32, name="kept", tag="mid")
         for c in range(CHUNKS):
             nc.tensor.transpose(lat_t[:, c, :], lat_sb[:, c * CHUNK : (c + 1) * CHUNK], ident[:])
         for c in range(CHUNKS):
             nc.scalar.activation(kept_t[:, c, :], lat_t[:, c, :], COPY, scale=coef_col[:, c, 0:1])
-        for c in range(2):
-            nc.tensor.transpose(kept[:, c * CHUNK : (c + 1) * CHUNK], kept_t[:, 2 + c, :], ident[:])
 
         pre = held.tile([P, CHUNKS, PACK, CHUNK], F32, name="pre")
         h_bf = held.tile([P, CHUNKS, PACK * CHUNK], BF16, name="h_bf", align_bytes=64)
@@ -193,9 +195,12 @@ def tile_picked_yddpm_relu_p_kernel(tc, x_words, x_scales, w1, w2, temb, lat, cs
         quantise_hidden(2)
         quantise_hidden(LAST)
 
+        kept = psum_h.tile([P, HALF], F32, name="kept", tag="wide")
+        for c in range(2):
+            nc.tensor.transpose(kept[:, c * CHUNK : (c + 1) * CHUNK], kept_t[:, 2 + c, :], ident[:])
         totals = [psum_h.tile([P, CHUNK], F32, name="total%d" % c, tag="wide") for c in range(2)]
         for c in range(2):
-            noise_t = psum_h.tile([P, N], F32, name="noise_t", tag="wide")
+            noise_t = psum_mid.tile([P, N], F32, name="noise_t", tag="mid")
             second_product(noise_t[:], c, True)
             nc.scalar.activation(removed_t[:, c, :], noise_t[:], COPY, scale=neg_noise_col[:, c : c + 1])
         for c in range(2):

@@ -27,6 +27,8 @@ HALF = S // 2
 LAST = CHUNKS - 1
 WINDOW = 704
 LANES = 16
+TURNED = (1, 0)
+DIRECT = (2, 3)
 
 
 def tile_picked_yddpm_relu_p_kernel(tc, x_words, x_scales, w1, w2, temb, lat, csig, cnoise, offs, step, out):
@@ -69,9 +71,9 @@ def tile_picked_yddpm_relu_p_kernel(tc, x_words, x_scales, w1, w2, temb, lat, cs
             )
         nc.sync.dma_start(offs_list[:], offs)
         nc.sync.dma_start(word_table[:], x_words[0].rearrange("p n t -> p (n t)").bitcast(I32))
+        nc.sync.dma_start(w2_raw[:], w2.rearrange("(p j) m -> p j m", j=PACK))
         nc.sync.dma_start(lat_sb[:], lat)
         nc.sync.dma_start(emb_last[:, :R], temb_rows[:, (PACK - 1) * R :])
-        nc.sync.dma_start(w2_raw[:], w2.rearrange("(p j) m -> p j m", j=PACK))
 
         coef_g = held.tile([P, S], F32, name="coef_g")
         nc.vector.tensor_copy(coef_g[:], coef[:].indirect(step_list[:]))
@@ -108,25 +110,27 @@ def tile_picked_yddpm_relu_p_kernel(tc, x_words, x_scales, w1, w2, temb, lat, cs
             nc.tensor.transpose(coef_t[:, c, :], coef_g[:, c * CHUNK : (c + 1) * CHUNK], ident[:])
         coef_col = held.tile([P, CHUNKS, 2], F32, name="coef_col")
         nc.scalar.copy(coef_col[:], coef_t[:, :, 0 : P : P // 2])
-        neg_noise_col = held.tile([P, 2], F32, name="neg_noise_col")
-        nc.scalar.activation(neg_noise_col[:], coef_t[:, :2, P // 2], COPY, scale=-1.0)
+        neg_noise_col = held.tile([P, CHUNKS], F32, name="neg_noise_col")
+        nc.scalar.activation(neg_noise_col[:], coef_t[:, :, P // 2], COPY, scale=-1.0)
         noise_ps = psum_mid.tile([P, HALF], F32, name="noise_ps", tag="mid")
-        for c in range(2):
+        for n, c in enumerate(DIRECT):
             nc.tensor.transpose(
-                noise_ps[:, c * CHUNK : (c + 1) * CHUNK], coef_col[:, 2 + c, 1:2].to_broadcast([P, P]), ident[:]
+                noise_ps[:, n * CHUNK : (n + 1) * CHUNK], coef_col[:, c, 1:2].to_broadcast([P, P]), ident[:]
             )
         noise_factor = held.tile([P, HALF], F32, name="noise_factor")
         nc.scalar.copy(noise_factor[:], noise_ps[:])
 
-        w2_bf = held.tile([P, N, PACK], BF16, name="w2_bf", align_bytes=64)
+        pre = held.tile([P, CHUNKS, PACK, CHUNK], F32, name="pre", align_bytes=64)
+        h_bf = held.tile([P, CHUNKS, PACK * CHUNK], BF16, name="h_bf", align_bytes=64)
+        w2_bf = h_bf[:, 0, :].rearrange("p (m j) -> p m j", j=PACK)
         nc.scalar.copy(
-            w2_bf[:].rearrange("p (a i) j -> p a j i", i=4),
+            w2_bf.rearrange("p (a i) j -> p a j i", i=4),
             w2_raw[:].rearrange("p j (a i) -> p a j i", i=4),
         )
         w2_codes = held.tile([P, N], U32, name="w2_codes", align_bytes=64)
         w2_sc = held.tile([P, N], U8, name="w2_sc", align_bytes=64)
         nc.vector.quantize_mx(
-            out=w2_codes[:].bitcast(FP8X4), scales=w2_sc[:], in_=w2_bf[:].rearrange("p m j -> p (m j)")
+            out=w2_codes[:].bitcast(FP8X4), scales=w2_sc[:], in_=w2_bf.rearrange("p m j -> p (m j)")
         )
 
         lat_t = psum_mid.tile([P, CHUNKS, P], F32, name="lat_t", tag="mid")
@@ -136,8 +140,7 @@ def tile_picked_yddpm_relu_p_kernel(tc, x_words, x_scales, w1, w2, temb, lat, cs
         for c in range(CHUNKS):
             nc.scalar.activation(kept_t[:, c, :], lat_t[:, c, :], COPY, scale=coef_col[:, c, 0:1])
 
-        pre = held.tile([P, CHUNKS, PACK, CHUNK], F32, name="pre")
-        h_bf = held.tile([P, CHUNKS, PACK * CHUNK], BF16, name="h_bf", align_bytes=64)
+        product_sb = held.tile([P, CHUNK, PACK], F32, name="product_sb")
         h_codes = held.tile([P, S], U32, name="h_codes", align_bytes=64)
         h_sc = held.tile([P, S], U8, name="h_sc", align_bytes=64)
         removed_t = held.tile([P, 2, N], F32, name="removed_t")
@@ -184,37 +187,40 @@ def tile_picked_yddpm_relu_p_kernel(tc, x_words, x_scales, w1, w2, temb, lat, cs
             )
 
         accs = [first_product(c) for c in range(CHUNKS)]
-        for c in range(CHUNKS):
+        nc.scalar.copy(product_sb[:], accs[0][:].rearrange("p t n -> p n t"))
+        nc.gpsimd.tensor_tensor(
+            h_bf[:, 0, :].rearrange("p (n t) -> p n t", t=PACK), product_sb[:], emb_g[:, :, :CHUNK].rearrange("p t n -> p n t"), ADD
+        )
+        for c in range(1, CHUNKS):
             nc.vector.tensor_tensor(pre[:, c], accs[c][:], emb_g[:, :, c * CHUNK : (c + 1) * CHUNK], ADD)
-            if c < LAST:
-                nc.scalar.activation(*relu_views(c), RELU)
-            if c >= 2:
-                quantise_hidden(c - 2)
+        for c in (1, 2):
+            nc.scalar.activation(*relu_views(c), RELU)
         nc.scalar.activation(*relu_views(LAST, 0, CHUNK // 2), RELU)
+        nc.vector.tensor_scalar_max(h_bf[:, 0, :], h_bf[:, 0, :], 0.0)
+        quantise_hidden(1)
         nc.vector.tensor_scalar_max(*relu_views(LAST, CHUNK // 2, CHUNK // 2), 0.0)
-        quantise_hidden(2)
-        quantise_hidden(LAST)
+        for c in (0, 2, LAST):
+            quantise_hidden(c)
 
         kept = psum_h.tile([P, HALF], F32, name="kept", tag="wide")
-        for c in range(2):
-            nc.tensor.transpose(kept[:, c * CHUNK : (c + 1) * CHUNK], kept_t[:, 2 + c, :], ident[:])
-        totals = [psum_h.tile([P, CHUNK], F32, name="total%d" % c, tag="wide") for c in range(2)]
-        for c in range(2):
+        for n, c in enumerate(DIRECT):
+            nc.tensor.transpose(kept[:, n * CHUNK : (n + 1) * CHUNK], kept_t[:, c, :], ident[:])
+        totals = [psum_h.tile([P, CHUNK], F32, name="total%d" % c, tag="wide") for c in TURNED]
+        for n, c in enumerate(TURNED):
             noise_t = psum_mid.tile([P, N], F32, name="noise_t", tag="mid")
             second_product(noise_t[:], c, True)
-            nc.scalar.activation(removed_t[:, c, :], noise_t[:], COPY, scale=neg_noise_col[:, c : c + 1])
-        for c in range(2):
-            cols = slice(c * CHUNK, (c + 1) * CHUNK)
+            nc.scalar.activation(removed_t[:, n, :], noise_t[:], COPY, scale=neg_noise_col[:, c : c + 1])
+        for n, c in enumerate(DIRECT):
+            cols = slice(n * CHUNK, (n + 1) * CHUNK)
             noise = psum_mid.tile([P, CHUNK], F32, name="noise", tag="mid")
-            second_product(noise[:], 2 + c, False)
+            second_product(noise[:], c, False)
             nc.vector.tensor_tensor(removed[:, cols], noise[:], noise_factor[:, cols], MULT)
-        for c in range(2):
-            cols = slice(c * CHUNK, (c + 1) * CHUNK)
-            nc.vector.tensor_tensor(result[:, HALF:][:, cols], kept[:, cols], removed[:, cols], SUBTRACT)
-        for c in range(2):
-            nc.tensor.matmul(totals[c][:], kept_t[:, c, :], ident[:], start=True, stop=False, is_transpose=True)
-            nc.tensor.matmul(totals[c][:], removed_t[:, c, :], ident[:], start=False, stop=True, is_transpose=True)
-            nc.scalar.copy(result[:, c * CHUNK : (c + 1) * CHUNK], totals[c][:])
-        nc.sync.dma_start(out[:, :HALF], result[:, :HALF])
-        for c in range(2, CHUNKS):
+        for n, c in enumerate(DIRECT):
+            cols = slice(n * CHUNK, (n + 1) * CHUNK)
+            nc.vector.tensor_tensor(result[:, c * CHUNK : (c + 1) * CHUNK], kept[:, cols], removed[:, cols], SUBTRACT)
             nc.sync.dma_start(out[:, c * CHUNK : (c + 1) * CHUNK], result[:, c * CHUNK : (c + 1) * CHUNK])
+        for n, c in enumerate(TURNED):
+            nc.tensor.matmul(totals[n][:], kept_t[:, c, :], ident[:], start=True, stop=False, is_transpose=True)
+            nc.tensor.matmul(totals[n][:], removed_t[:, n, :], ident[:], start=False, stop=True, is_transpose=True)
+            nc.scalar.copy(result[:, c * CHUNK : (c + 1) * CHUNK], totals[n][:])
+        nc.sync.dma_start(out[:, :HALF], result[:, :HALF])

@@ -41,26 +41,26 @@ def tile_picked_yddpm_relu_p_kernel(tc, x_words, x_scales, w1, w2, temb, lat, cs
         step_list = held.tile([P, S // LANES], U16, name="step_list")
         offs_list = held.tile([P, S // LANES], U16, name="offs_list")
         coef = held.tile([P, WINDOW], F32, name="coef")
-        emb = held.tile([P, (PACK - 2) * R + WINDOW], F32, name="emb")
-        emb_last = held.tile([P, WINDOW], F32, name="emb_last")
+        emb = held.tile([P, (PACK - 1) * R + WINDOW], F32, name="emb")
         scale_table = held.tile([P, T], U8, name="scale_table")
         word_table = held.tile([P, T], I32, name="word_table")
         w1_raw = [held.tile([P, PACK, H // 2], F32, name="w1_raw%d" % u) for u in range(2)]
-        w2_raw = held.tile([P, PACK, N], F32, name="w2_raw")
+        shared = held.tile([P, 2 * S], F32, name="shared")
+        w2_raw = shared[:, HALF : HALF + PACK * N].rearrange("p (j m) -> p j m", j=PACK)
         lat_sb = held.tile([P, S], F32, name="lat_sb")
         ident = held.tile([P, P], F32, name="ident")
 
         nc.gpsimd.memset(scale_table[:].bitcast(I32), 0)
+        nc.vector.memset(emb[:, PACK * R :], 0.0)
         nc.vector.memset(coef[:, R:], 0.0)
-        nc.vector.memset(emb[:, (PACK - 1) * R :], 0.0)
-        nc.vector.memset(emb_last[:, R:], 0.0)
         make_identity(nc, ident[:])
 
         nc.sync.dma_start(step_list[:], step)
+        temb_rows = temb.rearrange("(p t) r -> p (t r)", t=PACK)
+        nc.sync.dma_start(emb[:, 3 * R : 4 * R], temb_rows[:, 3 * R :])
         nc.sync.dma_start(coef[: P // 2, :R], csig[: P // 2, :])
         nc.sync.dma_start(coef[P // 2 :, :R], cnoise[P // 2 :, :])
-        temb_rows = temb.rearrange("(p t) r -> p (t r)", t=PACK)
-        nc.sync.dma_start(emb[:, : (PACK - 1) * R], temb_rows[:, : (PACK - 1) * R])
+        nc.sync.dma_start(emb[:, R : 3 * R], temb_rows[:, R : 3 * R])
         w1_rows = w1.rearrange("(p j) c -> p j c", j=PACK)
         for u in range(2):
             nc.sync.dma_start(w1_raw[u][:], w1_rows[:, :, u * H // 2 : (u + 1) * H // 2])
@@ -71,17 +71,21 @@ def tile_picked_yddpm_relu_p_kernel(tc, x_words, x_scales, w1, w2, temb, lat, cs
             )
         nc.sync.dma_start(offs_list[:], offs)
         nc.sync.dma_start(word_table[:], x_words[0].rearrange("p n t -> p (n t)").bitcast(I32))
-        nc.sync.dma_start(w2_raw[:], w2.rearrange("(p j) m -> p j m", j=PACK))
         nc.sync.dma_start(lat_sb[:], lat)
-        nc.sync.dma_start(emb_last[:, :R], temb_rows[:, (PACK - 1) * R :])
+        nc.sync.dma_start(w2_raw, w2.rearrange("(p j) m -> p j m", j=PACK))
+        nc.sync.dma_start(emb[:, :R], temb_rows[:, :R])
 
         coef_g = held.tile([P, S], F32, name="coef_g")
-        nc.vector.tensor_copy(coef_g[:], coef[:].indirect(step_list[:]))
-        staging = held.tile([P, (PACK + 1) * S], F32, name="staging", align_bytes=64)
-        emb_g = staging[:, : PACK * S].rearrange("p (t s) -> p t s", t=PACK)
-        w1_bf = staging[:, (PACK - 1) * S :].bitcast(BF16)
-        for t in range(PACK - 1):
+        emb_g = held.tile([P, PACK, S], F32, name="emb_g", align_bytes=64)
+        w1_bf = held.tile([P, PACK * H], BF16, name="w1_bf", align_bytes=64)[:]
+
+        def gather_plane(t):
             nc.vector.tensor_copy(emb_g[:, t, :], emb[:, t * R : t * R + WINDOW].indirect(step_list[:]))
+
+        gather_plane(3)
+        nc.vector.tensor_copy(coef_g[:], coef[:].indirect(step_list[:]))
+        for t in (2, 1):
+            gather_plane(t)
         x_sc = held.tile([P, S], U8, name="x_sc", align_bytes=64)
         nc.vector.tensor_copy(x_sc[:], scale_table[:].indirect(offs_list[:]))
 
@@ -103,15 +107,14 @@ def tile_picked_yddpm_relu_p_kernel(tc, x_words, x_scales, w1, w2, temb, lat, cs
                 x_codes[:, half * HALF : (half + 1) * HALF],
                 word_table[:].bitcast(U32).indirect(offs_list[:, entries]),
             )
-        nc.vector.tensor_copy(emb_g[:, PACK - 1, :], emb_last[:].indirect(step_list[:]))
 
         coef_t = psum_mid.tile([P, CHUNKS, P], F32, name="coef_t", tag="mid")
         for c in range(CHUNKS):
             nc.tensor.transpose(coef_t[:, c, :], coef_g[:, c * CHUNK : (c + 1) * CHUNK], ident[:])
-        coef_col = held.tile([P, CHUNKS, 2], F32, name="coef_col")
-        nc.scalar.copy(coef_col[:], coef_t[:, :, 0 : P : P // 2])
-        neg_noise_col = held.tile([P, CHUNKS], F32, name="neg_noise_col")
-        nc.scalar.activation(neg_noise_col[:], coef_t[:, :, P // 2], COPY, scale=-1.0)
+        coef_col = w1_raw[1][:, 0, : 2 * CHUNKS].rearrange("p (c s) -> p c s", s=2)
+        nc.scalar.copy(coef_col, coef_t[:, :, 0 : P : P // 2])
+        neg_noise_col = w1_raw[1][:, 0, 2 * CHUNKS : 3 * CHUNKS]
+        nc.scalar.activation(neg_noise_col, coef_t[:, :, P // 2], COPY, scale=-1.0)
         noise_ps = psum_mid.tile([P, HALF], F32, name="noise_ps", tag="mid")
         for n, c in enumerate(DIRECT):
             nc.tensor.transpose(
@@ -120,27 +123,26 @@ def tile_picked_yddpm_relu_p_kernel(tc, x_words, x_scales, w1, w2, temb, lat, cs
         noise_factor = held.tile([P, HALF], F32, name="noise_factor")
         nc.scalar.copy(noise_factor[:], noise_ps[:])
 
-        pre = held.tile([P, CHUNKS, PACK, CHUNK], F32, name="pre", align_bytes=64)
-        h_bf = held.tile([P, CHUNKS, PACK * CHUNK], BF16, name="h_bf", align_bytes=64)
-        w2_bf = h_bf[:, 0, :].rearrange("p (m j) -> p m j", j=PACK)
+        pre = {c: held.tile([P, PACK, CHUNK], F32, name="pre%d" % c) for c in range(1, CHUNKS)}
+        h_bf = [held.tile([P, PACK * CHUNK], BF16, name="h_bf%d" % c, align_bytes=64) for c in range(CHUNKS)]
+        w2_bf = emb_g[:, 0, : PACK * N // 2].bitcast(BF16).rearrange("p (m j) -> p m j", j=PACK)
         nc.scalar.copy(
             w2_bf.rearrange("p (a i) j -> p a j i", i=4),
-            w2_raw[:].rearrange("p j (a i) -> p a j i", i=4),
+            w2_raw.rearrange("p j (a i) -> p a j i", i=4),
         )
         w2_codes = held.tile([P, N], U32, name="w2_codes", align_bytes=64)
         w2_sc = held.tile([P, N], U8, name="w2_sc", align_bytes=64)
         nc.vector.quantize_mx(
             out=w2_codes[:].bitcast(FP8X4), scales=w2_sc[:], in_=w2_bf.rearrange("p m j -> p (m j)")
         )
+        gather_plane(0)
 
         lat_t = psum_mid.tile([P, CHUNKS, P], F32, name="lat_t", tag="mid")
-        kept_t = held.tile([P, CHUNKS, N], F32, name="kept_t")
+        kept_t = shared[:, S:].rearrange("p (c m) -> p c m", c=CHUNKS)
         for c in range(CHUNKS):
             nc.tensor.transpose(lat_t[:, c, :], lat_sb[:, c * CHUNK : (c + 1) * CHUNK], ident[:])
-        for c in range(CHUNKS):
-            nc.scalar.activation(kept_t[:, c, :], lat_t[:, c, :], COPY, scale=coef_col[:, c, 0:1])
 
-        product_sb = held.tile([P, CHUNK, PACK], F32, name="product_sb")
+        product_sb = shared[:, :S].rearrange("p (n t) -> p n t", t=PACK)
         h_codes = held.tile([P, S], U32, name="h_codes", align_bytes=64)
         h_sc = held.tile([P, S], U8, name="h_sc", align_bytes=64)
         removed_t = held.tile([P, 2, N], F32, name="removed_t")
@@ -165,16 +167,16 @@ def tile_picked_yddpm_relu_p_kernel(tc, x_words, x_scales, w1, w2, temb, lat, cs
 
         def relu_views(c, first=0, count=CHUNK):
             return (
-                h_bf[:, c, PACK * first : PACK * (first + count)].rearrange("p (a i t) -> p a t i", i=4, t=PACK),
-                pre[:, c, :, first : first + count].rearrange("p t (a i) -> p a t i", i=4),
+                h_bf[c][:, PACK * first : PACK * (first + count)].rearrange("p (a i t) -> p a t i", i=4, t=PACK),
+                pre[c][:, :, first : first + count].rearrange("p t (a i) -> p a t i", i=4),
             )
 
-        def quantise_hidden(c, count=1):
-            cols = slice(c * CHUNK, (c + count) * CHUNK)
+        def quantise_hidden(c):
+            cols = slice(c * CHUNK, (c + 1) * CHUNK)
             nc.vector.quantize_mx(
                 out=h_codes[:, cols].bitcast(FP8X4),
                 scales=h_sc[:, cols],
-                in_=h_bf[:, c : c + count, :].rearrange("p c w -> p (c w)"),
+                in_=h_bf[c][:],
             )
 
         def second_product(dst, c, tokens_on_partitions):
@@ -187,16 +189,18 @@ def tile_picked_yddpm_relu_p_kernel(tc, x_words, x_scales, w1, w2, temb, lat, cs
             )
 
         accs = [first_product(c) for c in range(CHUNKS)]
-        nc.scalar.copy(product_sb[:], accs[0][:].rearrange("p t n -> p n t"))
+        nc.scalar.copy(product_sb, accs[0][:].rearrange("p t n -> p n t"))
+        for c in range(CHUNKS):
+            nc.scalar.activation(kept_t[:, c, :], lat_t[:, c, :], COPY, scale=coef_col[:, c, 0:1])
         nc.gpsimd.tensor_tensor(
-            h_bf[:, 0, :].rearrange("p (n t) -> p n t", t=PACK), product_sb[:], emb_g[:, :, :CHUNK].rearrange("p t n -> p n t"), ADD
+            h_bf[0][:].rearrange("p (n t) -> p n t", t=PACK), product_sb, emb_g[:, :, :CHUNK].rearrange("p t n -> p n t"), ADD
         )
         for c in range(1, CHUNKS):
-            nc.vector.tensor_tensor(pre[:, c], accs[c][:], emb_g[:, :, c * CHUNK : (c + 1) * CHUNK], ADD)
+            nc.vector.tensor_tensor(pre[c][:], accs[c][:], emb_g[:, :, c * CHUNK : (c + 1) * CHUNK], ADD)
         for c in (1, 2):
             nc.scalar.activation(*relu_views(c), RELU)
         nc.scalar.activation(*relu_views(LAST, 0, CHUNK // 2), RELU)
-        nc.vector.tensor_scalar_max(h_bf[:, 0, :], h_bf[:, 0, :], 0.0)
+        nc.vector.tensor_scalar_max(h_bf[0][:], h_bf[0][:], 0.0)
         quantise_hidden(1)
         nc.vector.tensor_scalar_max(*relu_views(LAST, CHUNK // 2, CHUNK // 2), 0.0)
         for c in (0, 2, LAST):

@@ -27,6 +27,8 @@ HALF = S // 2
 LAST = CHUNKS - 1
 WINDOW = 704
 LANES = 16
+SIG_ROW, NOISE_ROW = 126, 127
+PLANE_AT = (0, 1, 2, 4)
 TURNED = (1, 0)
 DIRECT = (2, 3)
 
@@ -40,8 +42,8 @@ def tile_picked_yddpm_relu_p_kernel(tc, x_words, x_scales, w1, w2, temb, lat, cs
 
         step_list = held.tile([P, S // LANES], U16, name="step_list")
         offs_list = held.tile([P, S // LANES], U16, name="offs_list")
-        coef = held.tile([P, WINDOW], F32, name="coef")
-        emb = held.tile([P, (PACK - 1) * R + WINDOW], F32, name="emb")
+        tables = held.tile([P, PACK * R + WINDOW], F32, name="tables")
+        coef = tables[:, 3 * R : 3 * R + WINDOW]
         scale_table = held.tile([P, T], U8, name="scale_table")
         word_table = held.tile([P, T], I32, name="word_table")
         w1_raw = [held.tile([P, PACK, H // 2], F32, name="w1_raw%d" % u) for u in range(2)]
@@ -51,16 +53,16 @@ def tile_picked_yddpm_relu_p_kernel(tc, x_words, x_scales, w1, w2, temb, lat, cs
         ident = held.tile([P, P], F32, name="ident")
 
         nc.gpsimd.memset(scale_table[:].bitcast(I32), 0)
-        nc.vector.memset(emb[:, PACK * R :], 0.0)
-        nc.vector.memset(coef[:, R:], 0.0)
+        nc.vector.memset(tables[:, (PACK + 1) * R :], 0.0)
+        nc.vector.memset(coef[:SIG_ROW, :R], 0.0)
         make_identity(nc, ident[:])
 
         nc.sync.dma_start(step_list[:], step)
         temb_rows = temb.rearrange("(p t) r -> p (t r)", t=PACK)
-        nc.sync.dma_start(emb[:, 3 * R : 4 * R], temb_rows[:, 3 * R :])
-        nc.sync.dma_start(coef[: P // 2, :R], csig[: P // 2, :])
-        nc.sync.dma_start(coef[P // 2 :, :R], cnoise[P // 2 :, :])
-        nc.sync.dma_start(emb[:, R : 3 * R], temb_rows[:, R : 3 * R])
+        nc.sync.dma_start(tables[:, 4 * R : 5 * R], temb_rows[:, 3 * R :])
+        nc.sync.dma_start(coef[SIG_ROW : SIG_ROW + 1, :R], csig[0:1, :])
+        nc.sync.dma_start(coef[NOISE_ROW : NOISE_ROW + 1, :R], cnoise[0:1, :])
+        nc.sync.dma_start(tables[:, R : 3 * R], temb_rows[:, R : 3 * R])
         w1_rows = w1.rearrange("(p j) c -> p j c", j=PACK)
         for u in range(2):
             nc.sync.dma_start(w1_raw[u][:], w1_rows[:, :, u * H // 2 : (u + 1) * H // 2])
@@ -73,17 +75,18 @@ def tile_picked_yddpm_relu_p_kernel(tc, x_words, x_scales, w1, w2, temb, lat, cs
         nc.sync.dma_start(word_table[:], x_words[0].rearrange("p n t -> p (n t)").bitcast(I32))
         nc.sync.dma_start(lat_sb[:], lat)
         nc.sync.dma_start(w2_raw, w2.rearrange("(p j) m -> p j m", j=PACK))
-        nc.sync.dma_start(emb[:, :R], temb_rows[:, :R])
+        nc.sync.dma_start(tables[:, :R], temb_rows[:, :R])
 
         coef_g = held.tile([P, S], F32, name="coef_g")
         emb_g = held.tile([P, PACK, S], F32, name="emb_g", align_bytes=64)
         w1_bf = held.tile([P, PACK * H], BF16, name="w1_bf", align_bytes=64)[:]
 
         def gather_plane(t):
-            nc.vector.tensor_copy(emb_g[:, t, :], emb[:, t * R : t * R + WINDOW].indirect(step_list[:]))
+            first = PLANE_AT[t] * R
+            nc.vector.tensor_copy(emb_g[:, t, :], tables[:, first : first + WINDOW].indirect(step_list[:]))
 
         gather_plane(3)
-        nc.vector.tensor_copy(coef_g[:], coef[:].indirect(step_list[:]))
+        nc.vector.tensor_copy(coef_g[:], coef.indirect(step_list[:]))
         for t in (2, 1):
             gather_plane(t)
         x_sc = held.tile([P, S], U8, name="x_sc", align_bytes=64)
@@ -112,9 +115,9 @@ def tile_picked_yddpm_relu_p_kernel(tc, x_words, x_scales, w1, w2, temb, lat, cs
         for c in range(CHUNKS):
             nc.tensor.transpose(coef_t[:, c, :], coef_g[:, c * CHUNK : (c + 1) * CHUNK], ident[:])
         coef_col = w1_raw[1][:, 0, : 2 * CHUNKS].rearrange("p (c s) -> p c s", s=2)
-        nc.scalar.copy(coef_col, coef_t[:, :, 0 : P : P // 2])
+        nc.scalar.copy(coef_col, coef_t[:, :, SIG_ROW:])
         neg_noise_col = w1_raw[1][:, 0, 2 * CHUNKS : 3 * CHUNKS]
-        nc.scalar.activation(neg_noise_col, coef_t[:, :, P // 2], COPY, scale=-1.0)
+        nc.scalar.activation(neg_noise_col, coef_t[:, :, NOISE_ROW], COPY, scale=-1.0)
         noise_ps = psum_mid.tile([P, HALF], F32, name="noise_ps", tag="mid")
         for n, c in enumerate(DIRECT):
             nc.tensor.transpose(

@@ -37,8 +37,7 @@ def tile_picked_yddpm_relu_p_kernel(tc, x_words, x_scales, w1, w2, temb, lat, cs
     nc = tc.nc
     with ExitStack() as ctx:
         held = ctx.enter_context(tc.tile_pool(name="held", bufs=1))
-        psum_h = ctx.enter_context(tc.psum_pool(name="psum_h", bufs=CHUNKS))
-        psum_mid = ctx.enter_context(tc.psum_pool(name="psum_mid", bufs=4))
+        psum = ctx.enter_context(tc.psum_pool(name="psum", bufs=1))
 
         step_list = held.tile([P, S // LANES], U16, name="step_list")
         offs_list = held.tile([P, S // LANES], U16, name="offs_list")
@@ -47,14 +46,14 @@ def tile_picked_yddpm_relu_p_kernel(tc, x_words, x_scales, w1, w2, temb, lat, cs
         scale_table = held.tile([P, T], U8, name="scale_table")
         word_table = held.tile([P, T], I32, name="word_table")
         w1_raw = [held.tile([P, PACK, H // 2], F32, name="w1_raw%d" % u) for u in range(2)]
-        shared = held.tile([P, 2 * S], F32, name="shared")
+        shared = held.tile([P, 2 * S], F32, name="shared", tag="shared", align_bytes=64)
         w2_raw = shared[:, HALF : HALF + PACK * N].rearrange("p (j m) -> p j m", j=PACK)
         lat_sb = held.tile([P, S], F32, name="lat_sb")
         ident = held.tile([P, P], F32, name="ident")
 
+        nc.gpsimd.memset(tables[:, (PACK + 1) * R :], 0.0)
+        nc.gpsimd.memset(coef[:SIG_ROW, :R], 0.0)
         nc.gpsimd.memset(scale_table[:].bitcast(I32), 0)
-        nc.vector.memset(tables[:, (PACK + 1) * R :], 0.0)
-        nc.vector.memset(coef[:SIG_ROW, :R], 0.0)
         make_identity(nc, ident[:])
 
         nc.sync.dma_start(step_list[:], step)
@@ -111,14 +110,14 @@ def tile_picked_yddpm_relu_p_kernel(tc, x_words, x_scales, w1, w2, temb, lat, cs
                 word_table[:].bitcast(U32).indirect(offs_list[:, entries]),
             )
 
-        coef_t = psum_mid.tile([P, CHUNKS, P], F32, name="coef_t", tag="mid")
+        coef_t = psum.tile([P, CHUNKS, P], F32, name="coef_t", tag="b4")
         for c in range(CHUNKS):
             nc.tensor.transpose(coef_t[:, c, :], coef_g[:, c * CHUNK : (c + 1) * CHUNK], ident[:])
         coef_col = w1_raw[1][:, 0, : 2 * CHUNKS].rearrange("p (c s) -> p c s", s=2)
         nc.scalar.copy(coef_col, coef_t[:, :, SIG_ROW:])
         neg_noise_col = w1_raw[1][:, 0, 2 * CHUNKS : 3 * CHUNKS]
         nc.scalar.activation(neg_noise_col, coef_t[:, :, NOISE_ROW], COPY, scale=-1.0)
-        noise_ps = psum_mid.tile([P, HALF], F32, name="noise_ps", tag="mid")
+        noise_ps = psum.tile([P, HALF], F32, name="noise_ps", tag="b5")
         for n, c in enumerate(DIRECT):
             nc.tensor.transpose(
                 noise_ps[:, n * CHUNK : (n + 1) * CHUNK], coef_col[:, c, 1:2].to_broadcast([P, P]), ident[:]
@@ -128,24 +127,23 @@ def tile_picked_yddpm_relu_p_kernel(tc, x_words, x_scales, w1, w2, temb, lat, cs
 
         pre = {c: held.tile([P, PACK, CHUNK], F32, name="pre%d" % c) for c in range(1, CHUNKS)}
         h_bf = [held.tile([P, PACK * CHUNK], BF16, name="h_bf%d" % c, align_bytes=64) for c in range(CHUNKS)]
-        w2_bf = emb_g[:, 0, : PACK * N // 2].bitcast(BF16).rearrange("p (m j) -> p m j", j=PACK)
+        w2_cast = held.tile([P, PACK * N], BF16, name="w2_cast", align_bytes=64)
+        w2_bf = w2_cast[:].rearrange("p (m j) -> p m j", j=PACK)
         nc.scalar.copy(
             w2_bf.rearrange("p (a i) j -> p a j i", i=4),
             w2_raw.rearrange("p j (a i) -> p a j i", i=4),
         )
-        w2_codes = held.tile([P, N], U32, name="w2_codes", align_bytes=64)
-        w2_sc = held.tile([P, N], U8, name="w2_sc", align_bytes=64)
-        nc.vector.quantize_mx(
-            out=w2_codes[:].bitcast(FP8X4), scales=w2_sc[:], in_=w2_bf.rearrange("p m j -> p (m j)")
-        )
         gather_plane(0)
 
-        lat_t = psum_mid.tile([P, CHUNKS, P], F32, name="lat_t", tag="mid")
-        kept_t = shared[:, S:].rearrange("p (c m) -> p c m", c=CHUNKS)
+        lat_t = [psum.tile([P, P], F32, name="lat_t%d" % c, tag="b%d" % c) for c in range(CHUNKS)]
+        kept_t = held.tile([P, CHUNKS, N], F32, name="kept_t")
         for c in range(CHUNKS):
-            nc.tensor.transpose(lat_t[:, c, :], lat_sb[:, c * CHUNK : (c + 1) * CHUNK], ident[:])
+            nc.tensor.transpose(lat_t[c][:], lat_sb[:, c * CHUNK : (c + 1) * CHUNK], ident[:])
 
-        product_sb = shared[:, :S].rearrange("p (n t) -> p n t", t=PACK)
+        for c in range(CHUNKS):
+            nc.scalar.activation(kept_t[:, c, :], lat_t[c][:], COPY, scale=coef_col[:, c, 0:1])
+
+        product_sb = shared[:, :S].rearrange("p (a t i) -> p a t i", t=PACK, i=4)
         h_codes = held.tile([P, S], U32, name="h_codes", align_bytes=64)
         h_sc = held.tile([P, S], U8, name="h_sc", align_bytes=64)
         removed_t = held.tile([P, 2, N], F32, name="removed_t")
@@ -154,7 +152,7 @@ def tile_picked_yddpm_relu_p_kernel(tc, x_words, x_scales, w1, w2, temb, lat, cs
 
         def first_product(c):
             cols = slice(c * CHUNK, (c + 1) * CHUNK)
-            acc = psum_h.tile([P, PACK, CHUNK], F32, name="acc", tag="wide")
+            acc = psum.tile([P, PACK, CHUNK], F32, name="acc%d" % c, tag="b%d" % c)
             for t in range(PACK):
                 chans = slice(t * P, (t + 1) * P)
                 nc.tensor.matmul_mx(
@@ -192,34 +190,43 @@ def tile_picked_yddpm_relu_p_kernel(tc, x_words, x_scales, w1, w2, temb, lat, cs
             )
 
         accs = [first_product(c) for c in range(CHUNKS)]
-        nc.scalar.copy(product_sb, accs[0][:].rearrange("p t n -> p n t"))
-        for c in range(CHUNKS):
-            nc.scalar.activation(kept_t[:, c, :], lat_t[:, c, :], COPY, scale=coef_col[:, c, 0:1])
+        nc.scalar.copy(product_sb, accs[0][:].rearrange("p t (a i) -> p a t i", i=4))
         nc.gpsimd.tensor_tensor(
-            h_bf[0][:].rearrange("p (n t) -> p n t", t=PACK), product_sb, emb_g[:, :, :CHUNK].rearrange("p t n -> p n t"), ADD
+            h_bf[0][:].rearrange("p (a i t) -> p a t i", i=4, t=PACK),
+            product_sb,
+            emb_g[:, :, :CHUNK].rearrange("p t (a i) -> p a t i", i=4),
+            ADD,
         )
         for c in range(1, CHUNKS):
             nc.vector.tensor_tensor(pre[c][:], accs[c][:], emb_g[:, :, c * CHUNK : (c + 1) * CHUNK], ADD)
         for c in (1, 2):
             nc.scalar.activation(*relu_views(c), RELU)
         nc.scalar.activation(*relu_views(LAST, 0, CHUNK // 2), RELU)
+        w2_codes = held.tile([P, N], U32, name="w2_codes", tag="shared", align_bytes=64)
+        w2_sc = held.tile([P, N], U8, name="w2_sc", align_bytes=64)
+        nc.vector.quantize_mx(
+            out=w2_codes[:].bitcast(FP8X4), scales=w2_sc[:], in_=w2_bf.rearrange("p m j -> p (m j)")
+        )
         nc.vector.tensor_scalar_max(h_bf[0][:], h_bf[0][:], 0.0)
-        quantise_hidden(1)
+        for c in TURNED:
+            quantise_hidden(c)
         nc.vector.tensor_scalar_max(*relu_views(LAST, CHUNK // 2, CHUNK // 2), 0.0)
-        for c in (0, 2, LAST):
+        for c in DIRECT:
             quantise_hidden(c)
 
-        kept = psum_h.tile([P, HALF], F32, name="kept", tag="wide")
+        kept = psum.tile([P, HALF], F32, name="kept", tag="b0")
         for n, c in enumerate(DIRECT):
             nc.tensor.transpose(kept[:, n * CHUNK : (n + 1) * CHUNK], kept_t[:, c, :], ident[:])
-        totals = [psum_h.tile([P, CHUNK], F32, name="total%d" % c, tag="wide") for c in TURNED]
+        totals = [psum.tile([P, CHUNK], F32, name="total%d" % c, tag="b%d" % (2 - c)) for c in TURNED]
         for n, c in enumerate(TURNED):
-            noise_t = psum_mid.tile([P, N], F32, name="noise_t", tag="mid")
+            nc.tensor.matmul(totals[n][:], kept_t[:, c, :], ident[:], start=True, stop=False, is_transpose=True)
+        for n, c in enumerate(TURNED):
+            noise_t = psum.tile([P, N], F32, name="noise_t%d" % c, tag="b%d" % (4 + c))
             second_product(noise_t[:], c, True)
             nc.scalar.activation(removed_t[:, n, :], noise_t[:], COPY, scale=neg_noise_col[:, c : c + 1])
         for n, c in enumerate(DIRECT):
             cols = slice(n * CHUNK, (n + 1) * CHUNK)
-            noise = psum_mid.tile([P, CHUNK], F32, name="noise", tag="mid")
+            noise = psum.tile([P, CHUNK], F32, name="noise%d" % c, tag="b%d" % (4 + c))
             second_product(noise[:], c, False)
             nc.vector.tensor_tensor(removed[:, cols], noise[:], noise_factor[:, cols], MULT)
         for n, c in enumerate(DIRECT):
@@ -227,7 +234,6 @@ def tile_picked_yddpm_relu_p_kernel(tc, x_words, x_scales, w1, w2, temb, lat, cs
             nc.vector.tensor_tensor(result[:, c * CHUNK : (c + 1) * CHUNK], kept[:, cols], removed[:, cols], SUBTRACT)
             nc.sync.dma_start(out[:, c * CHUNK : (c + 1) * CHUNK], result[:, c * CHUNK : (c + 1) * CHUNK])
         for n, c in enumerate(TURNED):
-            nc.tensor.matmul(totals[n][:], kept_t[:, c, :], ident[:], start=True, stop=False, is_transpose=True)
             nc.tensor.matmul(totals[n][:], removed_t[:, n, :], ident[:], start=False, stop=True, is_transpose=True)
             nc.scalar.copy(result[:, c * CHUNK : (c + 1) * CHUNK], totals[n][:])
         nc.sync.dma_start(out[:, :HALF], result[:, :HALF])

@@ -28,7 +28,8 @@ LAST = CHUNKS - 1
 WINDOW = 704
 LANES = 16
 SIG_ROW, NOISE_ROW = 126, 127
-PLANE_AT = (0, 1, 2, 4)
+PLANE_AT = (1, 2, 4, 0)
+SCALE_ROWS = 112
 TURNED = (1, 0)
 DIRECT = (2, 3)
 
@@ -45,7 +46,11 @@ def tile_picked_yddpm_relu_p_kernel(tc, x_words, x_scales, w1, w2, temb, lat, cs
         coef = tables[:, 3 * R : 3 * R + WINDOW]
         scale_table = held.tile([P, T], U8, name="scale_table")
         word_table = held.tile([P, T], I32, name="word_table")
-        w1_raw = [held.tile([P, PACK, H // 2], F32, name="w1_raw%d" % u) for u in range(2)]
+        rows = held.tile([P, 2 * PACK - 1, S], F32, name="rows")
+        emb_g = rows[:, PACK - 1 :, :]
+        w1_first = held.tile([P, PACK, H // 2], F32, name="w1_first")
+        w1_raw = [w1_first[:], rows[:, :PACK, HALF:]]
+        x_sc = held.tile([P, S], U8, name="x_sc", align_bytes=64)
         shared = held.tile([P, 2 * S], F32, name="shared", tag="shared", align_bytes=64)
         w2_raw = shared[:, HALF : HALF + PACK * N].rearrange("p (j m) -> p j m", j=PACK)
         lat_sb = held.tile([P, S], F32, name="lat_sb")
@@ -53,56 +58,59 @@ def tile_picked_yddpm_relu_p_kernel(tc, x_words, x_scales, w1, w2, temb, lat, cs
 
         nc.gpsimd.memset(tables[:, (PACK + 1) * R :], 0.0)
         nc.gpsimd.memset(coef[:SIG_ROW, :R], 0.0)
-        nc.gpsimd.memset(scale_table[:].bitcast(I32), 0)
+        nc.gpsimd.memset(scale_table[:SCALE_ROWS, :].bitcast(I32), 0)
+        nc.gpsimd.memset(x_sc[:].bitcast(I32), 0)
         make_identity(nc, ident[:])
 
-        nc.sync.dma_start(step_list[:], step)
         temb_rows = temb.rearrange("(p t) r -> p (t r)", t=PACK)
-        nc.sync.dma_start(tables[:, 4 * R : 5 * R], temb_rows[:, 3 * R :])
+        nc.sync.dma_start(tables[:, 4 * R : 5 * R], temb_rows[:, 2 * R : 3 * R])
+        nc.sync.dma_start(step_list[:], step)
         nc.sync.dma_start(coef[SIG_ROW : SIG_ROW + 1, :R], csig[0:1, :])
         nc.sync.dma_start(coef[NOISE_ROW : NOISE_ROW + 1, :R], cnoise[0:1, :])
-        nc.sync.dma_start(tables[:, R : 3 * R], temb_rows[:, R : 3 * R])
+        nc.sync.dma_start(offs_list[:], offs)
+        nc.sync.dma_start(scale_table[SCALE_ROWS:, :].bitcast(I32), x_scales[0].bitcast(I32))
+        nc.sync.dma_start(tables[:, R : 3 * R], temb_rows[:, : 2 * R])
         w1_rows = w1.rearrange("(p j) c -> p j c", j=PACK)
         for u in range(2):
-            nc.sync.dma_start(w1_raw[u][:], w1_rows[:, :, u * H // 2 : (u + 1) * H // 2])
-        for q in range(4):
-            nc.sync.dma_start(
-                scale_table[32 * q : 32 * q + 4, :].bitcast(I32),
-                x_scales[0, 4 * q : 4 * q + 4, :].bitcast(I32),
-            )
-        nc.sync.dma_start(offs_list[:], offs)
+            nc.sync.dma_start(w1_raw[u], w1_rows[:, :, u * H // 2 : (u + 1) * H // 2])
         nc.sync.dma_start(word_table[:], x_words[0].rearrange("p n t -> p (n t)").bitcast(I32))
         nc.sync.dma_start(lat_sb[:], lat)
-        nc.sync.dma_start(w2_raw, w2.rearrange("(p j) m -> p j m", j=PACK))
-        nc.sync.dma_start(tables[:, :R], temb_rows[:, :R])
 
         coef_g = held.tile([P, S], F32, name="coef_g")
-        emb_g = held.tile([P, PACK, S], F32, name="emb_g", align_bytes=64)
-        w1_bf = held.tile([P, PACK * H], BF16, name="w1_bf", align_bytes=64)[:]
+        w1_bf = held.tile([P, PACK * H], BF16, name="w1_bf", tag="picked", align_bytes=64)[:]
 
-        def gather_plane(t):
-            first = PLANE_AT[t] * R
-            nc.vector.tensor_copy(emb_g[:, t, :], tables[:, first : first + WINDOW].indirect(step_list[:]))
+        def gather_plane(t, first=0, count=S):
+            window = tables[:, PLANE_AT[t] * R : PLANE_AT[t] * R + WINDOW]
+            entries = step_list[:, first // LANES : (first + count) // LANES]
+            nc.vector.tensor_copy(emb_g[:, t, first : first + count], window.indirect(entries))
 
-        gather_plane(3)
+        gather_plane(2)
         nc.vector.tensor_copy(coef_g[:], coef.indirect(step_list[:]))
-        for t in (2, 1):
-            gather_plane(t)
-        x_sc = held.tile([P, S], U8, name="x_sc", align_bytes=64)
-        nc.vector.tensor_copy(x_sc[:], scale_table[:].indirect(offs_list[:]))
+        picked_sc = held.tile([P, S], U8, name="picked_sc")
+        nc.vector.tensor_copy(picked_sc[:], scale_table[:].indirect(offs_list[:]))
+        for q in range(4):
+            nc.sync.dma_start(
+                x_sc[32 * q : 32 * q + 4, :].bitcast(I32),
+                picked_sc[SCALE_ROWS + 4 * q : SCALE_ROWS + 4 * q + 4, :].bitcast(I32),
+            )
+        nc.sync.dma_start(w2_raw, w2.rearrange("(p j) m -> p j m", j=PACK))
+        nc.sync.dma_start(tables[:, :R], temb_rows[:, 3 * R :])
+        gather_plane(1)
+        gather_plane(0, 0, HALF)
 
         for u in range(2):
             nc.scalar.copy(
                 w1_bf.rearrange("p (t m j) -> p m j t", t=PACK, j=PACK)[:, u * P // 2 : (u + 1) * P // 2],
-                w1_raw[u][:].rearrange("p j (m t) -> p m j t", t=PACK),
+                w1_raw[u].rearrange("p j (m t) -> p m j t", t=PACK),
             )
         w1_codes = held.tile([P, H], U32, name="w1_codes", align_bytes=64)
         w1_sc = held.tile([P, H], U8, name="w1_sc", align_bytes=64)
         nc.vector.quantize_mx(
             out=w1_codes[:].bitcast(FP8X4), scales=w1_sc[:], in_=w1_bf
         )
+        gather_plane(0, HALF, HALF)
 
-        x_codes = held.tile([P, S], U32, name="x_codes", align_bytes=64)
+        x_codes = held.tile([P, S], U32, name="x_codes", tag="picked", align_bytes=64)
         for half in range(2):
             entries = slice(half * HALF // LANES, (half + 1) * HALF // LANES)
             nc.vector.tensor_copy(
@@ -133,7 +141,7 @@ def tile_picked_yddpm_relu_p_kernel(tc, x_words, x_scales, w1, w2, temb, lat, cs
             w2_bf.rearrange("p (a i) j -> p a j i", i=4),
             w2_raw.rearrange("p j (a i) -> p a j i", i=4),
         )
-        gather_plane(0)
+        gather_plane(3)
 
         lat_t = [psum.tile([P, P], F32, name="lat_t%d" % c, tag="b%d" % c) for c in range(CHUNKS)]
         kept_t = held.tile([P, CHUNKS, N], F32, name="kept_t")

@@ -25,10 +25,9 @@ CHUNK = 128
 CHUNKS = S // CHUNK
 HALF = S // 2
 LAST = CHUNKS - 1
-WINDOW = 704
 LANES = 16
+WINDOW = R + LANES
 SIG_ROW, NOISE_ROW = 126, 127
-PLANE_AT = (1, 2, 4, 0)
 SCALE_ROWS = 112
 TURNED = (1, 0)
 DIRECT = (2, 3)
@@ -42,50 +41,55 @@ def tile_picked_yddpm_relu_p_kernel(tc, x_words, x_scales, w1, w2, temb, lat, cs
 
         step_list = held.tile([P, S // LANES], U16, name="step_list")
         offs_list = held.tile([P, S // LANES], U16, name="offs_list")
-        tables = held.tile([P, PACK * R + WINDOW], F32, name="tables")
-        coef = tables[:, 3 * R : 3 * R + WINDOW]
+        planes = [held.tile([P, WINDOW], F32, name="plane%d" % t) for t in range(PACK)]
+        coef = held.tile([P, WINDOW], F32, name="coef")
         scale_table = held.tile([P, T], U8, name="scale_table")
         word_table = held.tile([P, T], I32, name="word_table")
-        rows = held.tile([P, 2 * PACK - 1, S], F32, name="rows")
-        emb_g = rows[:, PACK - 1 :, :]
-        w1_first = held.tile([P, PACK, H // 2], F32, name="w1_first")
-        w1_raw = [w1_first[:], rows[:, :PACK, HALF:]]
+        emb_g = held.tile([P, PACK, S], F32, name="emb_g")
+        w1_raw = held.tile([P, PACK, H], F32, name="w1_raw", tag="raw")
         x_sc = held.tile([P, S], U8, name="x_sc", align_bytes=64)
-        shared = held.tile([P, 2 * S], F32, name="shared", tag="shared", align_bytes=64)
-        w2_raw = shared[:, HALF : HALF + PACK * N].rearrange("p (j m) -> p j m", j=PACK)
-        lat_sb = held.tile([P, S], F32, name="lat_sb")
         ident = held.tile([P, P], F32, name="ident")
 
-        nc.gpsimd.memset(tables[:, (PACK + 1) * R :], 0.0)
+        nc.gpsimd.memset(coef[:, R:], 0.0)
+        for t in range(PACK):
+            nc.scalar.activation(planes[t][:, R:], coef[:, R:], COPY)
         nc.gpsimd.memset(coef[:SIG_ROW, :R], 0.0)
         nc.gpsimd.memset(scale_table[:SCALE_ROWS, :].bitcast(I32), 0)
         nc.gpsimd.memset(x_sc[:].bitcast(I32), 0)
         make_identity(nc, ident[:])
 
-        temb_rows = temb.rearrange("(p t) r -> p (t r)", t=PACK)
-        nc.sync.dma_start(tables[:, 4 * R : 5 * R], temb_rows[:, 2 * R : 3 * R])
+        temb_rows = temb.rearrange("(p t) r -> p t r", t=PACK)
+        nc.sync.dma_start(planes[0][:, :R], temb_rows[:, 0, :])
         nc.sync.dma_start(step_list[:], step)
+        nc.sync.dma_start(planes[1][:, :R], temb_rows[:, 1, :])
         nc.sync.dma_start(coef[SIG_ROW : SIG_ROW + 1, :R], csig[0:1, :])
         nc.sync.dma_start(coef[NOISE_ROW : NOISE_ROW + 1, :R], cnoise[0:1, :])
         nc.sync.dma_start(offs_list[:], offs)
         nc.sync.dma_start(scale_table[SCALE_ROWS:, :].bitcast(I32), x_scales[0].bitcast(I32))
-        nc.sync.dma_start(tables[:, R : 3 * R], temb_rows[:, : 2 * R])
-        w1_rows = w1.rearrange("(p j) c -> p j c", j=PACK)
-        for u in range(2):
-            nc.sync.dma_start(w1_raw[u], w1_rows[:, :, u * H // 2 : (u + 1) * H // 2])
+        nc.sync.dma_start(w1_raw[:], w1.rearrange("(p j) c -> p j c", j=PACK))
+        nc.sync.dma_start(planes[2][:, :R], temb_rows[:, 2, :])
+        nc.sync.dma_start(planes[3][:, :R], temb_rows[:, 3, :])
         nc.sync.dma_start(word_table[:], x_words[0].rearrange("p n t -> p (n t)").bitcast(I32))
-        nc.sync.dma_start(lat_sb[:], lat)
 
+        def entries(lst, first, count):
+            return lst[:, first // LANES : (first + count) // LANES]
+
+        def scalar_lookup(dst, table):
+            for half in range(2):
+                nc.scalar.activation(
+                    dst[:, half * HALF : (half + 1) * HALF],
+                    table[:].indirect(entries(step_list, half * HALF, HALF)),
+                    COPY,
+                )
+
+        scalar_lookup(emb_g[:, 0, :], planes[0])
         coef_g = held.tile([P, S], F32, name="coef_g")
-        w1_bf = held.tile([P, PACK * H], BF16, name="w1_bf", tag="picked", align_bytes=64)[:]
-
-        def gather_plane(t, first=0, count=S):
-            window = tables[:, PLANE_AT[t] * R : PLANE_AT[t] * R + WINDOW]
-            entries = step_list[:, first // LANES : (first + count) // LANES]
-            nc.vector.tensor_copy(emb_g[:, t, first : first + count], window.indirect(entries))
-
-        gather_plane(2)
-        nc.vector.tensor_copy(coef_g[:], coef.indirect(step_list[:]))
+        scalar_lookup(coef_g, coef)
+        for half in range(2):
+            nc.vector.tensor_copy(
+                emb_g[:, 1, half * HALF : (half + 1) * HALF],
+                planes[1][:].indirect(entries(step_list, half * HALF, HALF)),
+            )
         picked_sc = held.tile([P, S], U8, name="picked_sc")
         nc.vector.tensor_copy(picked_sc[:], scale_table[:].indirect(offs_list[:]))
         for q in range(4):
@@ -93,38 +97,37 @@ def tile_picked_yddpm_relu_p_kernel(tc, x_words, x_scales, w1, w2, temb, lat, cs
                 x_sc[32 * q : 32 * q + 4, :].bitcast(I32),
                 picked_sc[SCALE_ROWS + 4 * q : SCALE_ROWS + 4 * q + 4, :].bitcast(I32),
             )
-        nc.sync.dma_start(w2_raw, w2.rearrange("(p j) m -> p j m", j=PACK))
-        nc.sync.dma_start(tables[:, :R], temb_rows[:, 3 * R :])
-        gather_plane(1)
-        gather_plane(0, 0, HALF)
+        scalar_lookup(emb_g[:, 2, :], planes[2])
+        scalar_lookup(emb_g[:, 3, :], planes[3])
 
-        for u in range(2):
-            nc.scalar.copy(
-                w1_bf.rearrange("p (t m j) -> p m j t", t=PACK, j=PACK)[:, u * P // 2 : (u + 1) * P // 2],
-                w1_raw[u].rearrange("p j (m t) -> p m j t", t=PACK),
-            )
+        w1_bf = held.tile([P, PACK * H], BF16, name="w1_bf", tag="cast", align_bytes=64)
+        nc.vector.tensor_copy(
+            w1_bf[:].rearrange("p (t m j) -> p m j t", t=PACK, j=PACK),
+            w1_raw[:].rearrange("p j (m t) -> p m j t", t=PACK),
+        )
         w1_codes = held.tile([P, H], U32, name="w1_codes", align_bytes=64)
         w1_sc = held.tile([P, H], U8, name="w1_sc", align_bytes=64)
-        nc.vector.quantize_mx(
-            out=w1_codes[:].bitcast(FP8X4), scales=w1_sc[:], in_=w1_bf
-        )
-        gather_plane(0, HALF, HALF)
+        nc.vector.quantize_mx(out=w1_codes[:].bitcast(FP8X4), scales=w1_sc[:], in_=w1_bf[:])
 
-        x_codes = held.tile([P, S], U32, name="x_codes", tag="picked", align_bytes=64)
-        for half in range(2):
-            entries = slice(half * HALF // LANES, (half + 1) * HALF // LANES)
+        w2_raw = held.tile([P, PACK, N], F32, name="w2_raw", tag="raw")
+        nc.sync.dma_start(w2_raw[:], w2.rearrange("(p j) m -> p j m", j=PACK))
+        lat_sb = held.tile([P, S], F32, name="lat_sb", tag="cast", align_bytes=64)
+        nc.sync.dma_start(lat_sb[:], lat)
+
+        x_codes = held.tile([P, S], U32, name="x_codes", align_bytes=64)
+        for first, count in ((0, CHUNK), (CHUNK, CHUNK), (HALF, HALF)):
             nc.vector.tensor_copy(
-                x_codes[:, half * HALF : (half + 1) * HALF],
-                word_table[:].bitcast(U32).indirect(offs_list[:, entries]),
+                x_codes[:, first : first + count],
+                word_table[:].bitcast(U32).indirect(entries(offs_list, first, count)),
             )
 
         coef_t = psum.tile([P, CHUNKS, P], F32, name="coef_t", tag="b4")
         for c in range(CHUNKS):
             nc.tensor.transpose(coef_t[:, c, :], coef_g[:, c * CHUNK : (c + 1) * CHUNK], ident[:])
-        coef_col = w1_raw[1][:, 0, : 2 * CHUNKS].rearrange("p (c s) -> p c s", s=2)
-        nc.scalar.copy(coef_col, coef_t[:, :, SIG_ROW:])
-        neg_noise_col = w1_raw[1][:, 0, 2 * CHUNKS : 3 * CHUNKS]
-        nc.scalar.activation(neg_noise_col, coef_t[:, :, NOISE_ROW], COPY, scale=-1.0)
+        coef_col = held.tile([P, CHUNKS, 2], F32, name="coef_col")
+        nc.scalar.copy(coef_col[:], coef_t[:, :, SIG_ROW:])
+        neg_noise_col = held.tile([P, CHUNKS], F32, name="neg_noise_col")
+        nc.scalar.activation(neg_noise_col[:], coef_t[:, :, NOISE_ROW], COPY, scale=-1.0)
         noise_ps = psum.tile([P, HALF], F32, name="noise_ps", tag="b5")
         for n, c in enumerate(DIRECT):
             nc.tensor.transpose(
@@ -133,25 +136,19 @@ def tile_picked_yddpm_relu_p_kernel(tc, x_words, x_scales, w1, w2, temb, lat, cs
         noise_factor = held.tile([P, HALF], F32, name="noise_factor")
         nc.scalar.copy(noise_factor[:], noise_ps[:])
 
+        w2_cast = held.tile([P, PACK * N], BF16, name="w2_cast", align_bytes=64)
+        nc.vector.tensor_copy(
+            w2_cast[:].rearrange("p (a i j) -> p a j i", i=4, j=PACK),
+            w2_raw[:].rearrange("p j (a i) -> p a j i", i=4),
+        )
+        w2_codes = held.tile([P, N], U32, name="w2_codes", align_bytes=64)
+        w2_sc = held.tile([P, N], U8, name="w2_sc", align_bytes=64)
+        nc.vector.quantize_mx(out=w2_codes[:].bitcast(FP8X4), scales=w2_sc[:], in_=w2_cast[:])
+
         pre = {c: held.tile([P, PACK, CHUNK], F32, name="pre%d" % c) for c in range(1, CHUNKS)}
         h_bf = [held.tile([P, PACK * CHUNK], BF16, name="h_bf%d" % c, align_bytes=64) for c in range(CHUNKS)]
-        w2_cast = held.tile([P, PACK * N], BF16, name="w2_cast", align_bytes=64)
-        w2_bf = w2_cast[:].rearrange("p (m j) -> p m j", j=PACK)
-        nc.scalar.copy(
-            w2_bf.rearrange("p (a i) j -> p a j i", i=4),
-            w2_raw.rearrange("p j (a i) -> p a j i", i=4),
-        )
-        gather_plane(3)
-
-        lat_t = [psum.tile([P, P], F32, name="lat_t%d" % c, tag="b%d" % c) for c in range(CHUNKS)]
-        kept_t = held.tile([P, CHUNKS, N], F32, name="kept_t")
-        for c in range(CHUNKS):
-            nc.tensor.transpose(lat_t[c][:], lat_sb[:, c * CHUNK : (c + 1) * CHUNK], ident[:])
-
-        for c in range(CHUNKS):
-            nc.scalar.activation(kept_t[:, c, :], lat_t[c][:], COPY, scale=coef_col[:, c, 0:1])
-
-        product_sb = shared[:, :S].rearrange("p (a t i) -> p a t i", t=PACK, i=4)
+        product = held.tile([P, PACK * CHUNK], F32, name="product")
+        product_sb = product[:].rearrange("p (a t i) -> p a t i", t=PACK, i=4)
         h_codes = held.tile([P, S], U32, name="h_codes", align_bytes=64)
         h_sc = held.tile([P, S], U8, name="h_sc", align_bytes=64)
         removed_t = held.tile([P, 2, N], F32, name="removed_t")
@@ -210,17 +207,19 @@ def tile_picked_yddpm_relu_p_kernel(tc, x_words, x_scales, w1, w2, temb, lat, cs
         for c in (1, 2):
             nc.scalar.activation(*relu_views(c), RELU)
         nc.scalar.activation(*relu_views(LAST, 0, CHUNK // 2), RELU)
-        w2_codes = held.tile([P, N], U32, name="w2_codes", tag="shared", align_bytes=64)
-        w2_sc = held.tile([P, N], U8, name="w2_sc", align_bytes=64)
-        nc.vector.quantize_mx(
-            out=w2_codes[:].bitcast(FP8X4), scales=w2_sc[:], in_=w2_bf.rearrange("p m j -> p (m j)")
-        )
         nc.vector.tensor_scalar_max(h_bf[0][:], h_bf[0][:], 0.0)
         for c in TURNED:
             quantise_hidden(c)
         nc.vector.tensor_scalar_max(*relu_views(LAST, CHUNK // 2, CHUNK // 2), 0.0)
         for c in DIRECT:
             quantise_hidden(c)
+
+        lat_t = psum.tile([P, CHUNKS, P], F32, name="lat_t", tag="b6")
+        kept_t = held.tile([P, CHUNKS, N], F32, name="kept_t")
+        for c in range(CHUNKS):
+            nc.tensor.transpose(lat_t[:, c, :], lat_sb[:, c * CHUNK : (c + 1) * CHUNK], ident[:])
+        for c in range(CHUNKS):
+            nc.scalar.activation(kept_t[:, c, :], lat_t[:, c, :], COPY, scale=coef_col[:, c, 0:1])
 
         kept = psum.tile([P, HALF], F32, name="kept", tag="b0")
         for n, c in enumerate(DIRECT):
@@ -234,7 +233,7 @@ def tile_picked_yddpm_relu_p_kernel(tc, x_words, x_scales, w1, w2, temb, lat, cs
             nc.scalar.activation(removed_t[:, n, :], noise_t[:], COPY, scale=neg_noise_col[:, c : c + 1])
         for n, c in enumerate(DIRECT):
             cols = slice(n * CHUNK, (n + 1) * CHUNK)
-            noise = psum.tile([P, CHUNK], F32, name="noise%d" % c, tag="b%d" % (4 + c))
+            noise = psum.tile([P, CHUNK], F32, name="noise%d" % c, tag=("b7", "b3")[n])
             second_product(noise[:], c, False)
             nc.vector.tensor_tensor(removed[:, cols], noise[:], noise_factor[:, cols], MULT)
         for n, c in enumerate(DIRECT):

@@ -27,9 +27,10 @@ HALF = S // 2
 LAST = CHUNKS - 1
 LANES = 16
 WINDOW = R + LANES
+PART_WINDOW = R + 96
 SIG_ROW, NOISE_ROW = 126, 127
 SCALE_ROWS = 112
-TURNED = (1, 0)
+TURNED = (0, 1)
 DIRECT = (2, 3)
 
 
@@ -37,59 +38,58 @@ def tile_picked_yddpm_relu_p_kernel(tc, x_words, x_scales, w1, w2, temb, lat, cs
     nc = tc.nc
     with ExitStack() as ctx:
         held = ctx.enter_context(tc.tile_pool(name="held", bufs=1))
+        reused = ctx.enter_context(tc.tile_pool(name="reused", bufs=1))
         psum = ctx.enter_context(tc.psum_pool(name="psum", bufs=1))
 
         step_list = held.tile([P, S // LANES], U16, name="step_list")
         offs_list = held.tile([P, S // LANES], U16, name="offs_list")
-        planes = [held.tile([P, WINDOW], F32, name="plane%d" % t) for t in range(PACK)]
+        early = held.tile([P, WINDOW], F32, name="early")
+        pair = held.tile([P, R + PART_WINDOW], F32, name="pair")
         coef = held.tile([P, WINDOW], F32, name="coef")
         scale_table = held.tile([P, T], U8, name="scale_table")
         word_table = held.tile([P, T], I32, name="word_table")
-        emb_g = held.tile([P, PACK, S], F32, name="emb_g")
-        w1_raw = held.tile([P, PACK, H], F32, name="w1_raw", tag="raw")
+        rows = held.tile([P, 2 * PACK - 1, HALF], F32, name="rows")
+        emb_first = held.tile([P, PACK, HALF], F32, name="emb_first", tag="emb0", align_bytes=64)
+        emb_g = [emb_first[:], rows[:, PACK - 1 :, :]]
+        w1_raw = [
+            reused.tile([P, PACK, H // 2], F32, name="w1_first", offset=0)[:],
+            rows[:, :PACK, :],
+        ]
         x_sc = held.tile([P, S], U8, name="x_sc", align_bytes=64)
         ident = held.tile([P, P], F32, name="ident")
 
         nc.gpsimd.memset(coef[:, R:], 0.0)
-        for t in range(PACK):
-            nc.scalar.activation(planes[t][:, R:], coef[:, R:], COPY)
+        nc.scalar.activation(early[:, R:], coef[:, R:], COPY)
+        nc.gpsimd.memset(pair[:, 2 * R :], 0.0)
         nc.gpsimd.memset(coef[:SIG_ROW, :R], 0.0)
         nc.gpsimd.memset(scale_table[:SCALE_ROWS, :].bitcast(I32), 0)
         nc.gpsimd.memset(x_sc[:].bitcast(I32), 0)
         make_identity(nc, ident[:])
 
         temb_rows = temb.rearrange("(p t) r -> p t r", t=PACK)
-        nc.sync.dma_start(planes[0][:, :R], temb_rows[:, 0, :])
+        nc.sync.dma_start(early[:, :R], temb_rows[:, 2, :])
         nc.sync.dma_start(step_list[:], step)
-        nc.sync.dma_start(planes[1][:, :R], temb_rows[:, 1, :])
-        nc.sync.dma_start(coef[SIG_ROW : SIG_ROW + 1, :R], csig[0:1, :])
-        nc.sync.dma_start(coef[NOISE_ROW : NOISE_ROW + 1, :R], cnoise[0:1, :])
         nc.sync.dma_start(offs_list[:], offs)
         nc.sync.dma_start(scale_table[SCALE_ROWS:, :].bitcast(I32), x_scales[0].bitcast(I32))
-        nc.sync.dma_start(w1_raw[:], w1.rearrange("(p j) c -> p j c", j=PACK))
-        nc.sync.dma_start(planes[2][:, :R], temb_rows[:, 2, :])
-        nc.sync.dma_start(planes[3][:, :R], temb_rows[:, 3, :])
+        w1_rows = w1.rearrange("(p j) c -> p j c", j=PACK)
+        nc.sync.dma_start(w1_raw[0], w1_rows[:, :, : H // 2])
+        nc.sync.dma_start(coef[SIG_ROW : SIG_ROW + 1, :R], csig[0:1, :])
+        nc.sync.dma_start(coef[NOISE_ROW : NOISE_ROW + 1, :R], cnoise[0:1, :])
+        nc.sync.dma_start(w1_raw[1], w1_rows[:, :, H // 2 :])
+        nc.sync.dma_start(pair[:, : 2 * R], temb.rearrange("(p t) r -> p (t r)", t=PACK)[:, : 2 * R])
         nc.sync.dma_start(word_table[:], x_words[0].rearrange("p n t -> p (n t)").bitcast(I32))
 
         def entries(lst, first, count):
             return lst[:, first // LANES : (first + count) // LANES]
 
-        def scalar_lookup(dst, table):
-            for half in range(2):
-                nc.scalar.activation(
-                    dst[:, half * HALF : (half + 1) * HALF],
-                    table[:].indirect(entries(step_list, half * HALF, HALF)),
-                    COPY,
-                )
+        def scalar_lookup(t, table, half):
+            nc.scalar.activation(emb_g[half][:, t, :], table[:].indirect(entries(step_list, half * HALF, HALF)), COPY)
 
-        scalar_lookup(emb_g[:, 0, :], planes[0])
-        coef_g = held.tile([P, S], F32, name="coef_g")
-        scalar_lookup(coef_g, coef)
+        def vector_lookup(dst, window, half):
+            nc.vector.tensor_copy(dst, window.indirect(entries(step_list, half * HALF, HALF)))
+
         for half in range(2):
-            nc.vector.tensor_copy(
-                emb_g[:, 1, half * HALF : (half + 1) * HALF],
-                planes[1][:].indirect(entries(step_list, half * HALF, HALF)),
-            )
+            scalar_lookup(2, early, half)
         picked_sc = held.tile([P, S], U8, name="picked_sc")
         nc.vector.tensor_copy(picked_sc[:], scale_table[:].indirect(offs_list[:]))
         for q in range(4):
@@ -97,22 +97,31 @@ def tile_picked_yddpm_relu_p_kernel(tc, x_words, x_scales, w1, w2, temb, lat, cs
                 x_sc[32 * q : 32 * q + 4, :].bitcast(I32),
                 picked_sc[SCALE_ROWS + 4 * q : SCALE_ROWS + 4 * q + 4, :].bitcast(I32),
             )
-        scalar_lookup(emb_g[:, 2, :], planes[2])
-        scalar_lookup(emb_g[:, 3, :], planes[3])
+        coef_g = held.tile([P, S], F32, name="coef_g")
+        for half in range(2):
+            vector_lookup(coef_g[:, half * HALF : (half + 1) * HALF], coef[:], half)
+        for half in range(2):
+            vector_lookup(emb_g[half][:, 1, :], pair[:, R:], half)
 
-        w1_bf = held.tile([P, PACK * H], BF16, name="w1_bf", tag="cast", align_bytes=64)
-        nc.vector.tensor_copy(
-            w1_bf[:].rearrange("p (t m j) -> p m j t", t=PACK, j=PACK),
-            w1_raw[:].rearrange("p j (m t) -> p m j t", t=PACK),
-        )
+        w1_bf = held.tile([P, PACK * H], BF16, name="w1_bf", align_bytes=64)
+        for u in range(2):
+            nc.scalar.copy(
+                w1_bf[:].rearrange("p (t m j) -> p m j t", t=PACK, j=PACK)[:, u * P // 2 : (u + 1) * P // 2],
+                w1_raw[u].rearrange("p j (m t) -> p m j t", t=PACK),
+            )
         w1_codes = held.tile([P, H], U32, name="w1_codes", align_bytes=64)
         w1_sc = held.tile([P, H], U8, name="w1_sc", align_bytes=64)
         nc.vector.quantize_mx(out=w1_codes[:].bitcast(FP8X4), scales=w1_sc[:], in_=w1_bf[:])
+        vector_lookup(emb_g[0][:, 0, :], pair[:], 0)
+        late = reused.tile([P, WINDOW], F32, name="late", offset=0)
+        nc.sync.dma_start(late[:, :R], temb_rows[:, 3, :])
+        nc.scalar.activation(late[:, R:], coef[:, R:], COPY)
 
-        w2_raw = held.tile([P, PACK, N], F32, name="w2_raw", tag="raw")
-        nc.sync.dma_start(w2_raw[:], w2.rearrange("(p j) m -> p j m", j=PACK))
-        lat_sb = held.tile([P, S], F32, name="lat_sb", tag="cast", align_bytes=64)
-        nc.sync.dma_start(lat_sb[:], lat)
+        tail_raw = reused.tile([P, PACK * N + S], F32, name="tail_raw", offset=4 * WINDOW)
+        w2_raw = tail_raw[:, : PACK * N].rearrange("p (j m) -> p j m", j=PACK)
+        lat_sb = tail_raw[:, PACK * N :]
+        nc.sync.dma_start(w2_raw, w2.rearrange("(p j) m -> p j m", j=PACK))
+        nc.sync.dma_start(lat_sb, lat)
 
         x_codes = held.tile([P, S], U32, name="x_codes", align_bytes=64)
         for first, count in ((0, CHUNK), (CHUNK, CHUNK), (HALF, HALF)):
@@ -124,31 +133,33 @@ def tile_picked_yddpm_relu_p_kernel(tc, x_words, x_scales, w1, w2, temb, lat, cs
         coef_t = psum.tile([P, CHUNKS, P], F32, name="coef_t", tag="b4")
         for c in range(CHUNKS):
             nc.tensor.transpose(coef_t[:, c, :], coef_g[:, c * CHUNK : (c + 1) * CHUNK], ident[:])
-        coef_col = held.tile([P, CHUNKS, 2], F32, name="coef_col")
-        nc.scalar.copy(coef_col[:], coef_t[:, :, SIG_ROW:])
-        neg_noise_col = held.tile([P, CHUNKS], F32, name="neg_noise_col")
-        nc.scalar.activation(neg_noise_col[:], coef_t[:, :, NOISE_ROW], COPY, scale=-1.0)
-        noise_ps = psum.tile([P, HALF], F32, name="noise_ps", tag="b5")
-        for n, c in enumerate(DIRECT):
-            nc.tensor.transpose(
-                noise_ps[:, n * CHUNK : (n + 1) * CHUNK], coef_col[:, c, 1:2].to_broadcast([P, P]), ident[:]
-            )
-        noise_factor = held.tile([P, HALF], F32, name="noise_factor")
-        nc.scalar.copy(noise_factor[:], noise_ps[:])
+        coef_col = w1_raw[1][:, 0, : 2 * CHUNKS].rearrange("p (c s) -> p c s", s=2)
+        nc.scalar.copy(coef_col, coef_t[:, :, SIG_ROW:])
+        neg_noise_col = w1_raw[1][:, 0, 2 * CHUNKS : 3 * CHUNKS]
+        nc.scalar.activation(neg_noise_col, coef_t[:, :, NOISE_ROW], COPY, scale=-1.0)
+        scalar_lookup(0, pair, 1)
+        factor_ps = psum.tile([P, 2, HALF], F32, name="factor_ps", tag="b5")
+        for s in range(2):
+            for n, c in enumerate(DIRECT):
+                nc.tensor.transpose(
+                    factor_ps[:, s, n * CHUNK : (n + 1) * CHUNK],
+                    coef_col[:, c, s : s + 1].to_broadcast([P, P]),
+                    ident[:],
+                )
+        factor = held.tile([P, 2, HALF], F32, name="factor")
+        nc.scalar.copy(factor[:], factor_ps[:])
+        noise_factor = factor[:, 1, :]
+        for half in range(2):
+            scalar_lookup(3, late, half)
 
         w2_cast = held.tile([P, PACK * N], BF16, name="w2_cast", align_bytes=64)
-        nc.vector.tensor_copy(
+        nc.scalar.copy(
             w2_cast[:].rearrange("p (a i j) -> p a j i", i=4, j=PACK),
-            w2_raw[:].rearrange("p j (a i) -> p a j i", i=4),
+            w2_raw.rearrange("p j (a i) -> p a j i", i=4),
         )
-        w2_codes = held.tile([P, N], U32, name="w2_codes", align_bytes=64)
-        w2_sc = held.tile([P, N], U8, name="w2_sc", align_bytes=64)
-        nc.vector.quantize_mx(out=w2_codes[:].bitcast(FP8X4), scales=w2_sc[:], in_=w2_cast[:])
 
-        pre = {c: held.tile([P, PACK, CHUNK], F32, name="pre%d" % c) for c in range(1, CHUNKS)}
+        pre = {c: held.tile([P, PACK, CHUNK], F32, name="pre%d" % c) for c in range(CHUNKS)}
         h_bf = [held.tile([P, PACK * CHUNK], BF16, name="h_bf%d" % c, align_bytes=64) for c in range(CHUNKS)]
-        product = held.tile([P, PACK * CHUNK], F32, name="product")
-        product_sb = product[:].rearrange("p (a t i) -> p a t i", t=PACK, i=4)
         h_codes = held.tile([P, S], U32, name="h_codes", align_bytes=64)
         h_sc = held.tile([P, S], U8, name="h_sc", align_bytes=64)
         removed_t = held.tile([P, 2, N], F32, name="removed_t")
@@ -195,36 +206,28 @@ def tile_picked_yddpm_relu_p_kernel(tc, x_words, x_scales, w1, w2, temb, lat, cs
             )
 
         accs = [first_product(c) for c in range(CHUNKS)]
-        nc.scalar.copy(product_sb, accs[0][:].rearrange("p t (a i) -> p a t i", i=4))
-        nc.gpsimd.tensor_tensor(
-            h_bf[0][:].rearrange("p (a i t) -> p a t i", i=4, t=PACK),
-            product_sb,
-            emb_g[:, :, :CHUNK].rearrange("p t (a i) -> p a t i", i=4),
-            ADD,
-        )
-        for c in range(1, CHUNKS):
-            nc.vector.tensor_tensor(pre[c][:], accs[c][:], emb_g[:, :, c * CHUNK : (c + 1) * CHUNK], ADD)
-        for c in (1, 2):
-            nc.scalar.activation(*relu_views(c), RELU)
-        nc.scalar.activation(*relu_views(LAST, 0, CHUNK // 2), RELU)
-        nc.vector.tensor_scalar_max(h_bf[0][:], h_bf[0][:], 0.0)
-        for c in TURNED:
-            quantise_hidden(c)
+        for c in range(CHUNKS):
+            half, first = divmod(c * CHUNK, HALF)
+            nc.vector.tensor_tensor(pre[c][:], accs[c][:], emb_g[half][:, :, first : first + CHUNK], ADD)
+            nc.scalar.activation(*relu_views(c, 0, CHUNK if c < LAST else CHUNK // 2), RELU)
+        w2_codes = held.tile([P, N], U32, name="w2_codes", tag="emb0", align_bytes=64)
+        w2_sc = held.tile([P, N], U8, name="w2_sc", align_bytes=64)
+        nc.vector.quantize_mx(out=w2_codes[:].bitcast(FP8X4), scales=w2_sc[:], in_=w2_cast[:])
+        quantise_hidden(0)
         nc.vector.tensor_scalar_max(*relu_views(LAST, CHUNK // 2, CHUNK // 2), 0.0)
-        for c in DIRECT:
+        for c in range(1, CHUNKS):
             quantise_hidden(c)
 
-        lat_t = psum.tile([P, CHUNKS, P], F32, name="lat_t", tag="b6")
-        kept_t = held.tile([P, CHUNKS, N], F32, name="kept_t")
-        for c in range(CHUNKS):
+        kept = held.tile([P, HALF], F32, name="kept")
+        nc.gpsimd.tensor_tensor(kept[:], lat_sb[:, HALF:], factor[:, 0, :], MULT)
+        lat_t = psum.tile([P, 2, P], F32, name="lat_t", tag="b6")
+        kept_t = held.tile([P, 2, N], F32, name="kept_t")
+        for c in TURNED:
             nc.tensor.transpose(lat_t[:, c, :], lat_sb[:, c * CHUNK : (c + 1) * CHUNK], ident[:])
-        for c in range(CHUNKS):
+        for c in TURNED:
             nc.scalar.activation(kept_t[:, c, :], lat_t[:, c, :], COPY, scale=coef_col[:, c, 0:1])
 
-        kept = psum.tile([P, HALF], F32, name="kept", tag="b0")
-        for n, c in enumerate(DIRECT):
-            nc.tensor.transpose(kept[:, n * CHUNK : (n + 1) * CHUNK], kept_t[:, c, :], ident[:])
-        totals = [psum.tile([P, CHUNK], F32, name="total%d" % c, tag="b%d" % (2 - c)) for c in TURNED]
+        totals = [psum.tile([P, CHUNK], F32, name="total%d" % c, tag="b%d" % c) for c in TURNED]
         for n, c in enumerate(TURNED):
             nc.tensor.matmul(totals[n][:], kept_t[:, c, :], ident[:], start=True, stop=False, is_transpose=True)
         for n, c in enumerate(TURNED):
@@ -233,7 +236,7 @@ def tile_picked_yddpm_relu_p_kernel(tc, x_words, x_scales, w1, w2, temb, lat, cs
             nc.scalar.activation(removed_t[:, n, :], noise_t[:], COPY, scale=neg_noise_col[:, c : c + 1])
         for n, c in enumerate(DIRECT):
             cols = slice(n * CHUNK, (n + 1) * CHUNK)
-            noise = psum.tile([P, CHUNK], F32, name="noise%d" % c, tag=("b7", "b3")[n])
+            noise = psum.tile([P, CHUNK], F32, name="noise%d" % c, tag=("b7", "b2")[n])
             second_product(noise[:], c, False)
             nc.vector.tensor_tensor(removed[:, cols], noise[:], noise_factor[:, cols], MULT)
         for n, c in enumerate(DIRECT):

@@ -27,7 +27,6 @@ HALF = S // 2
 LAST = CHUNKS - 1
 LANES = 16
 WINDOW = R + LANES
-PART_WINDOW = R + 96
 SIG_ROW, NOISE_ROW = 126, 127
 SCALE_ROWS = 112
 TURNED = (0, 1)
@@ -38,58 +37,54 @@ def tile_picked_yddpm_relu_p_kernel(tc, x_words, x_scales, w1, w2, temb, lat, cs
     nc = tc.nc
     with ExitStack() as ctx:
         held = ctx.enter_context(tc.tile_pool(name="held", bufs=1))
-        reused = ctx.enter_context(tc.tile_pool(name="reused", bufs=1))
         psum = ctx.enter_context(tc.psum_pool(name="psum", bufs=1))
 
         step_list = held.tile([P, S // LANES], U16, name="step_list")
         offs_list = held.tile([P, S // LANES], U16, name="offs_list")
-        early = held.tile([P, WINDOW], F32, name="early")
-        pair = held.tile([P, R + PART_WINDOW], F32, name="pair")
+        spare = (LANES, 3 * CHUNKS, LANES, S)
+        planes = [held.tile([P, R + spare[t]], F32, name="plane%d" % t) for t in range(LAST)]
         coef = held.tile([P, WINDOW], F32, name="coef")
-        scale_table = held.tile([P, T], U8, name="scale_table")
+        scale_table = held.tile([P, T], U8, name="scale_table", tag="scales")
         word_table = held.tile([P, T], I32, name="word_table")
-        rows = held.tile([P, 2 * PACK - 1, HALF], F32, name="rows")
-        emb_first = held.tile([P, PACK, HALF], F32, name="emb_first", tag="emb0", align_bytes=64)
-        emb_g = [emb_first[:], rows[:, PACK - 1 :, :]]
-        w1_raw = [
-            reused.tile([P, PACK, H // 2], F32, name="w1_first", offset=0)[:],
-            rows[:, :PACK, :],
+        emb_g = [
+            held.tile([P, PACK, HALF], F32, name="emb_g%d" % half, tag="emb%d" % half, align_bytes=64)
+            for half in range(2)
         ]
+        w1_raw = held.tile([P, PACK, H], F32, name="w1_raw", tag="raw")
         x_sc = held.tile([P, S], U8, name="x_sc", align_bytes=64)
         ident = held.tile([P, P], F32, name="ident")
 
         nc.gpsimd.memset(coef[:, R:], 0.0)
-        nc.scalar.activation(early[:, R:], coef[:, R:], COPY)
-        nc.gpsimd.memset(pair[:, 2 * R :], 0.0)
-        nc.gpsimd.memset(coef[:SIG_ROW, :R], 0.0)
+        for t in (2, 0):
+            nc.scalar.activation(planes[t][:, R:], coef[:, R:], COPY)
         nc.gpsimd.memset(scale_table[:SCALE_ROWS, :].bitcast(I32), 0)
+        nc.gpsimd.memset(coef[:SIG_ROW, :R], 0.0)
         nc.gpsimd.memset(x_sc[:].bitcast(I32), 0)
         make_identity(nc, ident[:])
 
         temb_rows = temb.rearrange("(p t) r -> p t r", t=PACK)
-        nc.sync.dma_start(early[:, :R], temb_rows[:, 2, :])
+        nc.sync.dma_start(planes[2][:, :R], temb_rows[:, 2, :])
         nc.sync.dma_start(step_list[:], step)
         nc.sync.dma_start(offs_list[:], offs)
         nc.sync.dma_start(scale_table[SCALE_ROWS:, :].bitcast(I32), x_scales[0].bitcast(I32))
-        w1_rows = w1.rearrange("(p j) c -> p j c", j=PACK)
-        nc.sync.dma_start(w1_raw[0], w1_rows[:, :, : H // 2])
+        nc.sync.dma_start(planes[0][:, :R], temb_rows[:, 0, :])
         nc.sync.dma_start(coef[SIG_ROW : SIG_ROW + 1, :R], csig[0:1, :])
         nc.sync.dma_start(coef[NOISE_ROW : NOISE_ROW + 1, :R], cnoise[0:1, :])
-        nc.sync.dma_start(w1_raw[1], w1_rows[:, :, H // 2 :])
-        nc.sync.dma_start(pair[:, : 2 * R], temb.rearrange("(p t) r -> p (t r)", t=PACK)[:, : 2 * R])
+        nc.sync.dma_start(w1_raw[:], w1.rearrange("(p j) c -> p j c", j=PACK))
+        nc.sync.dma_start(planes[1][:, :R], temb_rows[:, 1, :])
         nc.sync.dma_start(word_table[:], x_words[0].rearrange("p n t -> p (n t)").bitcast(I32))
 
         def entries(lst, first, count):
             return lst[:, first // LANES : (first + count) // LANES]
 
-        def scalar_lookup(t, table, half):
-            nc.scalar.activation(emb_g[half][:, t, :], table[:].indirect(entries(step_list, half * HALF, HALF)), COPY)
+        def plane_lookup(t, table):
+            for half in range(2):
+                nc.scalar.activation(
+                    emb_g[half][:, t, :], table[:].indirect(entries(step_list, half * HALF, HALF)), COPY
+                )
 
-        def vector_lookup(dst, window, half):
-            nc.vector.tensor_copy(dst, window.indirect(entries(step_list, half * HALF, HALF)))
-
-        for half in range(2):
-            scalar_lookup(2, early, half)
+        for t in (2, 0):
+            plane_lookup(t, planes[t])
         picked_sc = held.tile([P, S], U8, name="picked_sc")
         nc.vector.tensor_copy(picked_sc[:], scale_table[:].indirect(offs_list[:]))
         for q in range(4):
@@ -97,27 +92,24 @@ def tile_picked_yddpm_relu_p_kernel(tc, x_words, x_scales, w1, w2, temb, lat, cs
                 x_sc[32 * q : 32 * q + 4, :].bitcast(I32),
                 picked_sc[SCALE_ROWS + 4 * q : SCALE_ROWS + 4 * q + 4, :].bitcast(I32),
             )
+        late = held.tile([P, R + spare[LAST]], F32, name="late", tag="scales")
+        nc.sync.dma_start(late[:, :R], temb_rows[:, LAST, :])
         coef_g = held.tile([P, S], F32, name="coef_g")
         for half in range(2):
-            vector_lookup(coef_g[:, half * HALF : (half + 1) * HALF], coef[:], half)
-        for half in range(2):
-            vector_lookup(emb_g[half][:, 1, :], pair[:, R:], half)
+            nc.vector.tensor_copy(
+                coef_g[:, half * HALF : (half + 1) * HALF], coef[:].indirect(entries(step_list, half * HALF, HALF))
+            )
 
         w1_bf = held.tile([P, PACK * H], BF16, name="w1_bf", align_bytes=64)
-        for u in range(2):
-            nc.scalar.copy(
-                w1_bf[:].rearrange("p (t m j) -> p m j t", t=PACK, j=PACK)[:, u * P // 2 : (u + 1) * P // 2],
-                w1_raw[u].rearrange("p j (m t) -> p m j t", t=PACK),
-            )
+        nc.vector.tensor_copy(
+            w1_bf[:].rearrange("p (t m j) -> p m j t", t=PACK, j=PACK),
+            w1_raw[:].rearrange("p j (m t) -> p m j t", t=PACK),
+        )
         w1_codes = held.tile([P, H], U32, name="w1_codes", align_bytes=64)
         w1_sc = held.tile([P, H], U8, name="w1_sc", align_bytes=64)
         nc.vector.quantize_mx(out=w1_codes[:].bitcast(FP8X4), scales=w1_sc[:], in_=w1_bf[:])
-        vector_lookup(emb_g[0][:, 0, :], pair[:], 0)
-        late = reused.tile([P, WINDOW], F32, name="late", offset=0)
-        nc.sync.dma_start(late[:, :R], temb_rows[:, 3, :])
-        nc.scalar.activation(late[:, R:], coef[:, R:], COPY)
 
-        tail_raw = reused.tile([P, PACK * N + S], F32, name="tail_raw", offset=4 * WINDOW)
+        tail_raw = held.tile([P, PACK * N + S], F32, name="tail_raw", tag="raw")
         w2_raw = tail_raw[:, : PACK * N].rearrange("p (j m) -> p j m", j=PACK)
         lat_sb = tail_raw[:, PACK * N :]
         nc.sync.dma_start(w2_raw, w2.rearrange("(p j) m -> p j m", j=PACK))
@@ -133,11 +125,11 @@ def tile_picked_yddpm_relu_p_kernel(tc, x_words, x_scales, w1, w2, temb, lat, cs
         coef_t = psum.tile([P, CHUNKS, P], F32, name="coef_t", tag="b4")
         for c in range(CHUNKS):
             nc.tensor.transpose(coef_t[:, c, :], coef_g[:, c * CHUNK : (c + 1) * CHUNK], ident[:])
-        coef_col = w1_raw[1][:, 0, : 2 * CHUNKS].rearrange("p (c s) -> p c s", s=2)
+        coef_col = planes[1][:, R : R + 2 * CHUNKS].rearrange("p (c s) -> p c s", s=2)
         nc.scalar.copy(coef_col, coef_t[:, :, SIG_ROW:])
-        neg_noise_col = w1_raw[1][:, 0, 2 * CHUNKS : 3 * CHUNKS]
+        neg_noise_col = planes[1][:, R + 2 * CHUNKS :]
         nc.scalar.activation(neg_noise_col, coef_t[:, :, NOISE_ROW], COPY, scale=-1.0)
-        scalar_lookup(0, pair, 1)
+        plane_lookup(1, planes[1])
         factor_ps = psum.tile([P, 2, HALF], F32, name="factor_ps", tag="b5")
         for s in range(2):
             for n, c in enumerate(DIRECT):
@@ -146,14 +138,13 @@ def tile_picked_yddpm_relu_p_kernel(tc, x_words, x_scales, w1, w2, temb, lat, cs
                     coef_col[:, c, s : s + 1].to_broadcast([P, P]),
                     ident[:],
                 )
-        factor = held.tile([P, 2, HALF], F32, name="factor")
-        nc.scalar.copy(factor[:], factor_ps[:])
+        factor = late[:, R:].rearrange("p (s j) -> p s j", s=2)
+        nc.scalar.copy(factor, factor_ps[:])
         noise_factor = factor[:, 1, :]
-        for half in range(2):
-            scalar_lookup(3, late, half)
+        plane_lookup(LAST, late)
 
         w2_cast = held.tile([P, PACK * N], BF16, name="w2_cast", align_bytes=64)
-        nc.scalar.copy(
+        nc.vector.tensor_copy(
             w2_cast[:].rearrange("p (a i j) -> p a j i", i=4, j=PACK),
             w2_raw.rearrange("p j (a i) -> p a j i", i=4),
         )

@@ -144,9 +144,13 @@ def tile_picked_yddpm_relu_p_kernel(tc, x_words, x_scales, w1, w2, temb, lat, cs
         plane_lookup(LAST, late)
 
         w2_cast = held.tile([P, PACK * N], BF16, name="w2_cast", align_bytes=64)
-        nc.vector.tensor_copy(
+        nc.gpsimd.tensor_scalar(
             w2_cast[:].rearrange("p (a i j) -> p a j i", i=4, j=PACK),
             w2_raw.rearrange("p j (a i) -> p a j i", i=4),
+            1.0,
+            0.0,
+            MULT,
+            ADD,
         )
 
         pre = {c: held.tile([P, PACK, CHUNK], F32, name="pre%d" % c) for c in range(CHUNKS)}
@@ -157,13 +161,13 @@ def tile_picked_yddpm_relu_p_kernel(tc, x_words, x_scales, w1, w2, temb, lat, cs
         removed = held.tile([P, HALF], F32, name="removed")
         result = held.tile([P, S], F32, name="result")
 
-        def first_product(c):
+        def first_product(c, first, count, bank):
             cols = slice(c * CHUNK, (c + 1) * CHUNK)
-            acc = psum.tile([P, PACK, CHUNK], F32, name="acc%d" % c, tag="b%d" % c)
-            for t in range(PACK):
+            acc = psum.tile([P, count, CHUNK], F32, name="acc%d_%d" % (c, first), tag=bank)
+            for t in range(first, first + count):
                 chans = slice(t * P, (t + 1) * P)
                 nc.tensor.matmul_mx(
-                    out=acc[:, t, :],
+                    out=acc[:, t - first, :],
                     lhsT=w1_codes[:, chans].bitcast(FP8X4),
                     lhsT_scale=w1_sc[:, chans],
                     rhs=x_codes[:, cols].bitcast(FP8X4),
@@ -196,11 +200,14 @@ def tile_picked_yddpm_relu_p_kernel(tc, x_words, x_scales, w1, w2, temb, lat, cs
                 out=dst, lhsT=still[0], lhsT_scale=still[1], rhs=moving[0], rhs_scale=moving[1], start=True, stop=True
             )
 
-        accs = [first_product(c) for c in range(CHUNKS)]
-        for c in range(CHUNKS):
-            half, first = divmod(c * CHUNK, HALF)
-            nc.vector.tensor_tensor(pre[c][:], accs[c][:], emb_g[half][:, :, first : first + CHUNK], ADD)
-            nc.scalar.activation(*relu_views(c, 0, CHUNK if c < LAST else CHUNK // 2), RELU)
+        pieces = [(0, 0, 2, "b7"), (0, 2, 2, "b0")] + [(c, 0, PACK, "b%d" % c) for c in range(1, CHUNKS)]
+        accs = [first_product(*piece) for piece in pieces]
+        for acc, (c, first, count, bank) in zip(accs, pieces):
+            half, at = divmod(c * CHUNK, HALF)
+            tiles = slice(first, first + count)
+            nc.vector.tensor_tensor(pre[c][:, tiles, :], acc[:], emb_g[half][:, tiles, at : at + CHUNK], ADD)
+            if first + count == PACK:
+                nc.scalar.activation(*relu_views(c, 0, CHUNK if c < LAST else CHUNK // 2), RELU)
         w2_codes = held.tile([P, N], U32, name="w2_codes", tag="emb0", align_bytes=64)
         w2_sc = held.tile([P, N], U8, name="w2_sc", align_bytes=64)
         nc.vector.quantize_mx(out=w2_codes[:].bitcast(FP8X4), scales=w2_sc[:], in_=w2_cast[:])

@@ -41,8 +41,9 @@ def tile_picked_yddpm_relu_p_kernel(tc, x_words, x_scales, w1, w2, temb, lat, cs
 
         step_list = held.tile([P, S // LANES], U16, name="step_list")
         offs_list = held.tile([P, S // LANES], U16, name="offs_list")
-        spare = (LANES, 3 * CHUNKS, LANES, S)
-        planes = [held.tile([P, R + spare[t]], F32, name="plane%d" % t) for t in range(LAST)]
+        pair = held.tile([P, 2 * R], F32, name="pair")
+        second = held.tile([P, R + 3 * CHUNKS], F32, name="second")
+        third = held.tile([P, WINDOW], F32, name="third")
         coef = held.tile([P, WINDOW], F32, name="coef")
         scale_table = held.tile([P, T], U8, name="scale_table", tag="scales")
         word_table = held.tile([P, T], I32, name="word_table")
@@ -55,23 +56,21 @@ def tile_picked_yddpm_relu_p_kernel(tc, x_words, x_scales, w1, w2, temb, lat, cs
         ident = held.tile([P, P], F32, name="ident")
 
         nc.gpsimd.memset(coef[:, R:], 0.0)
-        for t in (2, 0):
-            nc.scalar.activation(planes[t][:, R:], coef[:, R:], COPY)
+        nc.scalar.activation(third[:, R:], coef[:, R:], COPY)
         nc.gpsimd.memset(scale_table[:SCALE_ROWS, :].bitcast(I32), 0)
         nc.gpsimd.memset(coef[:SIG_ROW, :R], 0.0)
         nc.gpsimd.memset(x_sc[:].bitcast(I32), 0)
         make_identity(nc, ident[:])
 
-        temb_rows = temb.rearrange("(p t) r -> p t r", t=PACK)
-        nc.sync.dma_start(planes[2][:, :R], temb_rows[:, 2, :])
+        temb_rows = temb.rearrange("(p t) r -> p (t r)", t=PACK)
+        nc.sync.dma_start(third[:, :R], temb_rows[:, 2 * R : 3 * R])
         nc.sync.dma_start(step_list[:], step)
         nc.sync.dma_start(offs_list[:], offs)
-        nc.sync.dma_start(scale_table[SCALE_ROWS:, :].bitcast(I32), x_scales[0].bitcast(I32))
-        nc.sync.dma_start(planes[0][:, :R], temb_rows[:, 0, :])
-        nc.sync.dma_start(coef[SIG_ROW : SIG_ROW + 1, :R], csig[0:1, :])
-        nc.sync.dma_start(coef[NOISE_ROW : NOISE_ROW + 1, :R], cnoise[0:1, :])
+        nc.scalar.dma_start(scale_table[SCALE_ROWS:, :].bitcast(I32), x_scales[0].bitcast(I32))
+        nc.sync.dma_start(pair[:], temb_rows[:, : 2 * R])
+        nc.scalar.dma_start(coef[SIG_ROW : SIG_ROW + 1, :R], csig[0:1, :])
+        nc.scalar.dma_start(coef[NOISE_ROW : NOISE_ROW + 1, :R], cnoise[0:1, :])
         nc.sync.dma_start(w1_raw[:], w1.rearrange("(p j) c -> p j c", j=PACK))
-        nc.sync.dma_start(planes[1][:, :R], temb_rows[:, 1, :])
         nc.sync.dma_start(word_table[:], x_words[0].rearrange("p n t -> p (n t)").bitcast(I32))
 
         def entries(lst, first, count):
@@ -83,8 +82,9 @@ def tile_picked_yddpm_relu_p_kernel(tc, x_words, x_scales, w1, w2, temb, lat, cs
                     emb_g[half][:, t, :], table[:].indirect(entries(step_list, half * HALF, HALF)), COPY
                 )
 
-        for t in (2, 0):
-            plane_lookup(t, planes[t])
+        plane_lookup(2, third)
+        plane_lookup(0, pair)
+        nc.scalar.copy(second[:, :R], pair[:, R:])
         picked_sc = held.tile([P, S], U8, name="picked_sc")
         nc.vector.tensor_copy(picked_sc[:], scale_table[:].indirect(offs_list[:]))
         for q in range(4):
@@ -92,8 +92,8 @@ def tile_picked_yddpm_relu_p_kernel(tc, x_words, x_scales, w1, w2, temb, lat, cs
                 x_sc[32 * q : 32 * q + 4, :].bitcast(I32),
                 picked_sc[SCALE_ROWS + 4 * q : SCALE_ROWS + 4 * q + 4, :].bitcast(I32),
             )
-        late = held.tile([P, R + spare[LAST]], F32, name="late", tag="scales")
-        nc.sync.dma_start(late[:, :R], temb_rows[:, LAST, :])
+        late = held.tile([P, R + S], F32, name="late", tag="scales")
+        nc.sync.dma_start(late[:, :R], temb_rows[:, LAST * R :])
         coef_g = held.tile([P, S], F32, name="coef_g")
         for half in range(2):
             nc.vector.tensor_copy(
@@ -125,11 +125,11 @@ def tile_picked_yddpm_relu_p_kernel(tc, x_words, x_scales, w1, w2, temb, lat, cs
         coef_t = psum.tile([P, CHUNKS, P], F32, name="coef_t", tag="b4")
         for c in range(CHUNKS):
             nc.tensor.transpose(coef_t[:, c, :], coef_g[:, c * CHUNK : (c + 1) * CHUNK], ident[:])
-        coef_col = planes[1][:, R : R + 2 * CHUNKS].rearrange("p (c s) -> p c s", s=2)
+        coef_col = second[:, R : R + 2 * CHUNKS].rearrange("p (c s) -> p c s", s=2)
         nc.scalar.copy(coef_col, coef_t[:, :, SIG_ROW:])
-        neg_noise_col = planes[1][:, R + 2 * CHUNKS :]
+        neg_noise_col = second[:, R + 2 * CHUNKS :]
         nc.scalar.activation(neg_noise_col, coef_t[:, :, NOISE_ROW], COPY, scale=-1.0)
-        plane_lookup(1, planes[1])
+        plane_lookup(1, second)
         factor_ps = psum.tile([P, 2, HALF], F32, name="factor_ps", tag="b5")
         for s in range(2):
             for n, c in enumerate(DIRECT):

@@ -56,35 +56,40 @@ def tile_picked_yddpm_relu_p_kernel(tc, x_words, x_scales, w1, w2, temb, lat, cs
         ident = held.tile([P, P], F32, name="ident")
 
         nc.gpsimd.memset(coef[:, R:], 0.0)
-        nc.scalar.activation(third[:, R:], coef[:, R:], COPY)
-        nc.gpsimd.memset(scale_table[:SCALE_ROWS, :].bitcast(I32), 0)
         nc.gpsimd.memset(coef[:SIG_ROW, :R], 0.0)
+        nc.gpsimd.memset(scale_table[:SCALE_ROWS, :].bitcast(I32), 0)
         nc.gpsimd.memset(x_sc[:].bitcast(I32), 0)
         make_identity(nc, ident[:])
 
         temb_rows = temb.rearrange("(p t) r -> p (t r)", t=PACK)
         nc.sync.dma_start(third[:, :R], temb_rows[:, 2 * R : 3 * R])
+        nc.scalar.dma_start(coef[SIG_ROW : SIG_ROW + 1, :R], csig[0:1, :])
+        nc.scalar.dma_start(coef[NOISE_ROW : NOISE_ROW + 1, :R], cnoise[0:1, :])
         nc.sync.dma_start(step_list[:], step)
         nc.sync.dma_start(offs_list[:], offs)
         nc.scalar.dma_start(scale_table[SCALE_ROWS:, :].bitcast(I32), x_scales[0].bitcast(I32))
+        nc.scalar.activation(third[:, R:], coef[:, R:], COPY)
         nc.sync.dma_start(pair[:], temb_rows[:, : 2 * R])
-        nc.scalar.dma_start(coef[SIG_ROW : SIG_ROW + 1, :R], csig[0:1, :])
-        nc.scalar.dma_start(coef[NOISE_ROW : NOISE_ROW + 1, :R], cnoise[0:1, :])
         nc.sync.dma_start(w1_raw[:], w1.rearrange("(p j) c -> p j c", j=PACK))
         nc.sync.dma_start(word_table[:], x_words[0].rearrange("p n t -> p (n t)").bitcast(I32))
 
         def entries(lst, first, count):
             return lst[:, first // LANES : (first + count) // LANES]
 
-        def plane_lookup(t, table):
-            for half in range(2):
+        def plane_lookup(t, table, halves=(0, 1)):
+            for half in halves:
                 nc.scalar.activation(
                     emb_g[half][:, t, :], table[:].indirect(entries(step_list, half * HALF, HALF)), COPY
                 )
 
         plane_lookup(2, third)
-        plane_lookup(0, pair)
+        plane_lookup(0, pair, (0,))
         nc.scalar.copy(second[:, :R], pair[:, R:])
+        coef_g = held.tile([P, S], F32, name="coef_g")
+        for half in range(2):
+            nc.vector.tensor_copy(
+                coef_g[:, half * HALF : (half + 1) * HALF], coef[:].indirect(entries(step_list, half * HALF, HALF))
+            )
         picked_sc = held.tile([P, S], U8, name="picked_sc")
         nc.vector.tensor_copy(picked_sc[:], scale_table[:].indirect(offs_list[:]))
         for q in range(4):
@@ -94,11 +99,7 @@ def tile_picked_yddpm_relu_p_kernel(tc, x_words, x_scales, w1, w2, temb, lat, cs
             )
         late = held.tile([P, R + S], F32, name="late", tag="scales")
         nc.sync.dma_start(late[:, :R], temb_rows[:, LAST * R :])
-        coef_g = held.tile([P, S], F32, name="coef_g")
-        for half in range(2):
-            nc.vector.tensor_copy(
-                coef_g[:, half * HALF : (half + 1) * HALF], coef[:].indirect(entries(step_list, half * HALF, HALF))
-            )
+        nc.vector.tensor_copy(emb_g[1][:, 0, :], pair[:].indirect(entries(step_list, HALF, HALF)))
 
         w1_bf = held.tile([P, PACK * H], BF16, name="w1_bf", align_bytes=64)
         nc.vector.tensor_copy(

@@ -29,8 +29,6 @@ LANES = 16
 WINDOW = R + LANES
 SIG_ROW, NOISE_ROW = 126, 127
 SCALE_ROWS = 112
-TURNED = (0, 1)
-DIRECT = (2, 3)
 
 
 def tile_picked_yddpm_relu_p_kernel(tc, x_words, x_scales, w1, w2, temb, lat, csig, cnoise, offs, step, out):
@@ -42,7 +40,7 @@ def tile_picked_yddpm_relu_p_kernel(tc, x_words, x_scales, w1, w2, temb, lat, cs
         step_list = held.tile([P, S // LANES], U16, name="step_list")
         offs_list = held.tile([P, S // LANES], U16, name="offs_list")
         pair = held.tile([P, 2 * R], F32, name="pair")
-        second = held.tile([P, R + 3 * CHUNKS], F32, name="second")
+        second = held.tile([P, R + 2 * CHUNKS], F32, name="second")
         third = held.tile([P, WINDOW], F32, name="third")
         coef = held.tile([P, WINDOW], F32, name="coef")
         scale_table = held.tile([P, T], U8, name="scale_table", tag="scales")
@@ -97,7 +95,7 @@ def tile_picked_yddpm_relu_p_kernel(tc, x_words, x_scales, w1, w2, temb, lat, cs
                 x_sc[32 * q : 32 * q + 4, :].bitcast(I32),
                 picked_sc[SCALE_ROWS + 4 * q : SCALE_ROWS + 4 * q + 4, :].bitcast(I32),
             )
-        late = held.tile([P, R + S], F32, name="late", tag="scales")
+        late = held.tile([P, R + 2 * S], F32, name="late", tag="scales")
         nc.sync.dma_start(late[:, :R], temb_rows[:, LAST * R :])
         nc.vector.tensor_copy(emb_g[1][:, 0, :], pair[:].indirect(entries(step_list, HALF, HALF)))
 
@@ -126,27 +124,26 @@ def tile_picked_yddpm_relu_p_kernel(tc, x_words, x_scales, w1, w2, temb, lat, cs
         coef_t = psum.tile([P, CHUNKS, P], F32, name="coef_t", tag="b4")
         for c in range(CHUNKS):
             nc.tensor.transpose(coef_t[:, c, :], coef_g[:, c * CHUNK : (c + 1) * CHUNK], ident[:])
-        coef_col = second[:, R : R + 2 * CHUNKS].rearrange("p (c s) -> p c s", s=2)
+        coef_col = second[:, R:].rearrange("p (c s) -> p c s", s=2)
         nc.scalar.copy(coef_col, coef_t[:, :, SIG_ROW:])
-        neg_noise_col = second[:, R + 2 * CHUNKS :]
-        nc.scalar.activation(neg_noise_col, coef_t[:, :, NOISE_ROW], COPY, scale=-1.0)
         plane_lookup(1, second)
-        factor_ps = psum.tile([P, 2, HALF], F32, name="factor_ps", tag="b5")
+        factor = late[:, R:].rearrange("p (s j) -> p s j", s=2)
         for s in range(2):
-            for n, c in enumerate(DIRECT):
+            factor_ps = psum.tile([P, S], F32, name="factor_ps%d" % s, tag="b%d" % (5 + s))
+            for c in range(CHUNKS):
                 nc.tensor.transpose(
-                    factor_ps[:, s, n * CHUNK : (n + 1) * CHUNK],
+                    factor_ps[:, c * CHUNK : (c + 1) * CHUNK],
                     coef_col[:, c, s : s + 1].to_broadcast([P, P]),
                     ident[:],
                 )
-        factor = late[:, R:].rearrange("p (s j) -> p s j", s=2)
-        nc.scalar.copy(factor, factor_ps[:])
-        noise_factor = factor[:, 1, :]
+            nc.scalar.copy(factor[:, s, :], factor_ps[:])
+        sig_factor, noise_factor = factor[:, 0, :], factor[:, 1, :]
         plane_lookup(LAST, late)
 
-        w2_cast = held.tile([P, PACK * N], BF16, name="w2_cast", align_bytes=64)
+        staged = held.tile([P, PACK * (N + S)], BF16, name="staged", align_bytes=64)
+        w2_cast = staged[:, : PACK * N]
         nc.gpsimd.tensor_scalar(
-            w2_cast[:].rearrange("p (a i j) -> p a j i", i=4, j=PACK),
+            w2_cast.rearrange("p (a i j) -> p a j i", i=4, j=PACK),
             w2_raw.rearrange("p j (a i) -> p a j i", i=4),
             1.0,
             0.0,
@@ -154,13 +151,10 @@ def tile_picked_yddpm_relu_p_kernel(tc, x_words, x_scales, w1, w2, temb, lat, cs
             ADD,
         )
 
-        pre = {c: held.tile([P, PACK, CHUNK], F32, name="pre%d" % c) for c in range(CHUNKS)}
-        h_bf = [held.tile([P, PACK * CHUNK], BF16, name="h_bf%d" % c, align_bytes=64) for c in range(CHUNKS)]
-        h_codes = held.tile([P, S], U32, name="h_codes", align_bytes=64)
-        h_sc = held.tile([P, S], U8, name="h_sc", align_bytes=64)
-        removed_t = held.tile([P, 2, N], F32, name="removed_t")
-        removed = held.tile([P, HALF], F32, name="removed")
-        result = held.tile([P, S], F32, name="result")
+        pre = [held.tile([P, PACK, CHUNK], F32, name="pre%d" % c, tag="pre%d" % c) for c in range(CHUNKS)]
+        h_bf = [staged[:, PACK * (N + c * CHUNK) : PACK * (N + (c + 1) * CHUNK)] for c in range(CHUNKS)]
+        codes = held.tile([P, N + S], U32, name="codes", tag="codes", align_bytes=64)
+        scales = held.tile([P, N + S], U8, name="code_scales", align_bytes=64)
 
         def first_product(c, first, count, bank):
             cols = slice(c * CHUNK, (c + 1) * CHUNK)
@@ -178,28 +172,32 @@ def tile_picked_yddpm_relu_p_kernel(tc, x_words, x_scales, w1, w2, temb, lat, cs
                 )
             return acc
 
-        def relu_views(c, first=0, count=CHUNK):
+        def relu_views(c):
             return (
-                h_bf[c][:, PACK * first : PACK * (first + count)].rearrange("p (a i t) -> p a t i", i=4, t=PACK),
-                pre[c][:, :, first : first + count].rearrange("p t (a i) -> p a t i", i=4),
+                h_bf[c].rearrange("p (a i t) -> p a t i", i=4, t=PACK),
+                pre[c][:].rearrange("p t (a i) -> p a t i", i=4),
             )
 
-        def quantise_hidden(c):
-            cols = slice(c * CHUNK, (c + 1) * CHUNK)
+        def quantise_staged(first, count):
             nc.vector.quantize_mx(
-                out=h_codes[:, cols].bitcast(FP8X4),
-                scales=h_sc[:, cols],
-                in_=h_bf[c][:],
+                out=codes[:, first : first + count].bitcast(FP8X4),
+                scales=scales[:, first : first + count],
+                in_=staged[:, PACK * first : PACK * (first + count)],
             )
 
-        def second_product(dst, c, tokens_on_partitions):
-            cols = slice(c * CHUNK, (c + 1) * CHUNK)
-            hidden = (h_codes[:, cols].bitcast(FP8X4), h_sc[:, cols])
-            weights = (w2_codes[:].bitcast(FP8X4), w2_sc[:])
-            still, moving = (hidden, weights) if tokens_on_partitions else (weights, hidden)
+        def second_product(c):
+            cols = slice(N + c * CHUNK, N + (c + 1) * CHUNK)
+            noise = psum.tile([P, CHUNK], F32, name="noise%d" % c, tag="b%d" % (4 + c))
             nc.tensor.matmul_mx(
-                out=dst, lhsT=still[0], lhsT_scale=still[1], rhs=moving[0], rhs_scale=moving[1], start=True, stop=True
+                out=noise[:],
+                lhsT=codes[:, :N].bitcast(FP8X4),
+                lhsT_scale=scales[:, :N],
+                rhs=codes[:, cols].bitcast(FP8X4),
+                rhs_scale=scales[:, cols],
+                start=True,
+                stop=True,
             )
+            return noise
 
         pieces = [(0, 0, 2, "b7"), (0, 2, 2, "b0")] + [(c, 0, PACK, "b%d" % c) for c in range(1, CHUNKS)]
         accs = [first_product(*piece) for piece in pieces]
@@ -208,41 +206,21 @@ def tile_picked_yddpm_relu_p_kernel(tc, x_words, x_scales, w1, w2, temb, lat, cs
             tiles = slice(first, first + count)
             nc.vector.tensor_tensor(pre[c][:, tiles, :], acc[:], emb_g[half][:, tiles, at : at + CHUNK], ADD)
             if first + count == PACK:
-                nc.scalar.activation(*relu_views(c, 0, CHUNK if c < LAST else CHUNK // 2), RELU)
-        w2_codes = held.tile([P, N], U32, name="w2_codes", tag="emb0", align_bytes=64)
-        w2_sc = held.tile([P, N], U8, name="w2_sc", align_bytes=64)
-        nc.vector.quantize_mx(out=w2_codes[:].bitcast(FP8X4), scales=w2_sc[:], in_=w2_cast[:])
-        quantise_hidden(0)
-        nc.vector.tensor_scalar_max(*relu_views(LAST, CHUNK // 2, CHUNK // 2), 0.0)
+                nc.scalar.activation(*relu_views(c), RELU)
+        quantise_staged(0, N + CHUNK)
         for c in range(1, CHUNKS):
-            quantise_hidden(c)
+            quantise_staged(N + c * CHUNK, CHUNK)
 
-        kept = held.tile([P, HALF], F32, name="kept")
-        nc.gpsimd.tensor_tensor(kept[:], lat_sb[:, HALF:], factor[:, 0, :], MULT)
-        lat_t = psum.tile([P, 2, P], F32, name="lat_t", tag="b6")
-        kept_t = held.tile([P, 2, N], F32, name="kept_t")
-        for c in TURNED:
-            nc.tensor.transpose(lat_t[:, c, :], lat_sb[:, c * CHUNK : (c + 1) * CHUNK], ident[:])
-        for c in TURNED:
-            nc.scalar.activation(kept_t[:, c, :], lat_t[:, c, :], COPY, scale=coef_col[:, c, 0:1])
-
-        totals = [psum.tile([P, CHUNK], F32, name="total%d" % c, tag="b%d" % c) for c in TURNED]
-        for n, c in enumerate(TURNED):
-            nc.tensor.matmul(totals[n][:], kept_t[:, c, :], ident[:], start=True, stop=False, is_transpose=True)
-        for n, c in enumerate(TURNED):
-            noise_t = psum.tile([P, N], F32, name="noise_t%d" % c, tag="b%d" % (4 + c))
-            second_product(noise_t[:], c, True)
-            nc.scalar.activation(removed_t[:, n, :], noise_t[:], COPY, scale=neg_noise_col[:, c : c + 1])
-        for n, c in enumerate(DIRECT):
-            cols = slice(n * CHUNK, (n + 1) * CHUNK)
-            noise = psum.tile([P, CHUNK], F32, name="noise%d" % c, tag=("b7", "b2")[n])
-            second_product(noise[:], c, False)
-            nc.vector.tensor_tensor(removed[:, cols], noise[:], noise_factor[:, cols], MULT)
-        for n, c in enumerate(DIRECT):
-            cols = slice(n * CHUNK, (n + 1) * CHUNK)
-            nc.vector.tensor_tensor(result[:, c * CHUNK : (c + 1) * CHUNK], kept[:, cols], removed[:, cols], SUBTRACT)
-            nc.sync.dma_start(out[:, c * CHUNK : (c + 1) * CHUNK], result[:, c * CHUNK : (c + 1) * CHUNK])
-        for n, c in enumerate(TURNED):
-            nc.tensor.matmul(totals[n][:], removed_t[:, n, :], ident[:], start=False, stop=True, is_transpose=True)
-            nc.scalar.copy(result[:, c * CHUNK : (c + 1) * CHUNK], totals[n][:])
-        nc.sync.dma_start(out[:, :HALF], result[:, :HALF])
+        kept = held.tile([P, S], F32, name="kept")
+        nc.gpsimd.tensor_tensor(kept[:], lat_sb, sig_factor, MULT)
+        removed = held.tile([P, S], F32, name="removed", tag="pre%d" % LAST)
+        for c in range(CHUNKS):
+            cols = slice(c * CHUNK, (c + 1) * CHUNK)
+            nc.vector.tensor_tensor(removed[:, cols], second_product(c)[:], noise_factor[:, cols], MULT)
+        early = held.tile([P, CHUNK], F32, name="early")
+        nc.gpsimd.tensor_tensor(early[:], kept[:, :CHUNK], removed[:, :CHUNK], SUBTRACT)
+        nc.sync.dma_start(out[:, :CHUNK], early[:])
+        result = held.tile([P, S], F32, name="result", tag="codes", align_bytes=64)
+        for cols in (slice(CHUNK, LAST * CHUNK), slice(LAST * CHUNK, S)):
+            nc.vector.tensor_tensor(result[:, cols], kept[:, cols], removed[:, cols], SUBTRACT)
+            nc.sync.dma_start(out[:, cols], result[:, cols])

@@ -100,13 +100,20 @@ def tile_picked_yddpm_relu_p_kernel(tc, x_words, x_scales, w1, w2, temb, lat, cs
         nc.vector.tensor_copy(emb_g[1][:, 0, :], pair[:].indirect(entries(step_list, HALF, HALF)))
 
         w1_bf = held.tile([P, PACK * H], BF16, name="w1_bf", align_bytes=64)
-        nc.vector.tensor_copy(
-            w1_bf[:].rearrange("p (t m j) -> p m j t", t=PACK, j=PACK),
-            w1_raw[:].rearrange("p j (m t) -> p m j t", t=PACK),
-        )
+        for tiles in (slice(0, 2), slice(2, PACK)):
+            nc.vector.tensor_copy(
+                w1_bf[:].rearrange("p (t m j) -> p m j t", t=PACK, j=PACK)[:, :, :, tiles],
+                w1_raw[:].rearrange("p j (m t) -> p m j t", t=PACK)[:, :, :, tiles],
+            )
         w1_codes = held.tile([P, H], U32, name="w1_codes", align_bytes=64)
         w1_sc = held.tile([P, H], U8, name="w1_sc", align_bytes=64)
-        nc.vector.quantize_mx(out=w1_codes[:].bitcast(FP8X4), scales=w1_sc[:], in_=w1_bf[:])
+        for first in (0, H // 2):
+            chans = slice(first, first + H // 2)
+            nc.vector.quantize_mx(
+                out=w1_codes[:, chans].bitcast(FP8X4),
+                scales=w1_sc[:, chans],
+                in_=w1_bf[:, PACK * first : PACK * (first + H // 2)],
+            )
 
         tail_raw = held.tile([P, PACK * N + S], F32, name="tail_raw", tag="raw")
         w2_raw = tail_raw[:, : PACK * N].rearrange("p (j m) -> p j m", j=PACK)

@@ -29,6 +29,7 @@ LANES = 16
 WINDOW = R + LANES
 SIG_ROW, NOISE_ROW = 126, 127
 SCALE_ROWS = 112
+W2_SPLIT = 32
 
 
 def tile_picked_yddpm_relu_p_kernel(tc, x_words, x_scales, w1, w2, temb, lat, csig, cnoise, offs, step, out):
@@ -149,9 +150,14 @@ def tile_picked_yddpm_relu_p_kernel(tc, x_words, x_scales, w1, w2, temb, lat, cs
 
         staged = held.tile([P, PACK * (N + S)], BF16, name="staged", align_bytes=64)
         w2_cast = staged[:, : PACK * N]
+        nc.scalar.activation(
+            w2_cast[:, : PACK * W2_SPLIT].rearrange("p (a i j) -> p a j i", i=4, j=PACK),
+            w2_raw[:, :, :W2_SPLIT].rearrange("p j (a i) -> p a j i", i=4),
+            COPY,
+        )
         nc.gpsimd.tensor_scalar(
-            w2_cast.rearrange("p (a i j) -> p a j i", i=4, j=PACK),
-            w2_raw.rearrange("p j (a i) -> p a j i", i=4),
+            w2_cast[:, PACK * W2_SPLIT :].rearrange("p (m j) -> p m j", j=PACK),
+            w2_raw[:, :, W2_SPLIT:].rearrange("p j m -> p m j"),
             1.0,
             0.0,
             MULT,

@@ -36,6 +36,7 @@ def tile_picked_yddpm_relu_p_kernel(tc, x_words, x_scales, w1, w2, temb, lat, cs
     nc = tc.nc
     with ExitStack() as ctx:
         held = ctx.enter_context(tc.tile_pool(name="held", bufs=1))
+        shared = ctx.enter_context(tc.tile_pool(name="shared", bufs=1))
         psum = ctx.enter_context(tc.psum_pool(name="psum", bufs=1))
 
         step_list = held.tile([P, S // LANES], U16, name="step_list")
@@ -44,7 +45,7 @@ def tile_picked_yddpm_relu_p_kernel(tc, x_words, x_scales, w1, w2, temb, lat, cs
         second = held.tile([P, R + 2 * CHUNKS], F32, name="second")
         third = held.tile([P, WINDOW], F32, name="third")
         coef = held.tile([P, WINDOW], F32, name="coef")
-        scale_table = held.tile([P, T], U8, name="scale_table", tag="scales")
+        scale_table = shared.tile([P, T], U8, name="scale_table", offset=3072)
         word_table = held.tile([P, T], I32, name="word_table")
         emb_g = [
             held.tile([P, PACK, HALF], F32, name="emb_g%d" % half, tag="emb%d" % half, align_bytes=64)
@@ -96,7 +97,7 @@ def tile_picked_yddpm_relu_p_kernel(tc, x_words, x_scales, w1, w2, temb, lat, cs
                 x_sc[32 * q : 32 * q + 4, :].bitcast(I32),
                 picked_sc[SCALE_ROWS + 4 * q : SCALE_ROWS + 4 * q + 4, :].bitcast(I32),
             )
-        late = held.tile([P, R + 2 * S], F32, name="late", tag="scales")
+        late = shared.tile([P, WINDOW], F32, name="late", offset=4096)
         nc.sync.dma_start(late[:, :R], temb_rows[:, LAST * R :])
         nc.vector.tensor_copy(emb_g[1][:, 0, :], pair[:].indirect(entries(step_list, HALF, HALF)))
 
@@ -135,7 +136,7 @@ def tile_picked_yddpm_relu_p_kernel(tc, x_words, x_scales, w1, w2, temb, lat, cs
         coef_col = second[:, R:].rearrange("p (c s) -> p c s", s=2)
         nc.scalar.copy(coef_col, coef_t[:, :, SIG_ROW:])
         plane_lookup(1, second)
-        factor = late[:, R:].rearrange("p (s j) -> p s j", s=2)
+        factor = held.tile([P, 2, S], F32, name="factor")
         for s in range(2):
             factor_ps = psum.tile([P, S], F32, name="factor_ps%d" % s, tag="b%d" % (5 + s))
             for c in range(CHUNKS):
@@ -146,6 +147,7 @@ def tile_picked_yddpm_relu_p_kernel(tc, x_words, x_scales, w1, w2, temb, lat, cs
                 )
             nc.scalar.copy(factor[:, s, :], factor_ps[:])
         sig_factor, noise_factor = factor[:, 0, :], factor[:, 1, :]
+        nc.scalar.copy(late[:, R:], factor_ps[:, :LANES])
         plane_lookup(LAST, late)
 
         staged = held.tile([P, PACK * (N + S)], BF16, name="staged", align_bytes=64)
@@ -164,7 +166,12 @@ def tile_picked_yddpm_relu_p_kernel(tc, x_words, x_scales, w1, w2, temb, lat, cs
             ADD,
         )
 
-        pre = [held.tile([P, PACK, CHUNK], F32, name="pre%d" % c, tag="pre%d" % c) for c in range(CHUNKS)]
+        pre = [
+            held.tile([P, PACK, CHUNK], F32, name="pre0"),
+            shared.tile([P, PACK, CHUNK], F32, name="pre1", offset=2112),
+            shared.tile([P, PACK, CHUNK], F32, name="pre2", offset=4160),
+            held.tile([P, PACK, CHUNK], F32, name="pre3", tag="emb0", align_bytes=64),
+        ]
         h_bf = [staged[:, PACK * (N + c * CHUNK) : PACK * (N + (c + 1) * CHUNK)] for c in range(CHUNKS)]
         codes = held.tile([P, N + S], U32, name="codes", tag="codes", align_bytes=64)
         scales = held.tile([P, N + S], U8, name="code_scales", align_bytes=64)
@@ -200,7 +207,7 @@ def tile_picked_yddpm_relu_p_kernel(tc, x_words, x_scales, w1, w2, temb, lat, cs
 
         def second_product(c):
             cols = slice(N + c * CHUNK, N + (c + 1) * CHUNK)
-            noise = psum.tile([P, CHUNK], F32, name="noise%d" % c, tag="b%d" % (4 + c))
+            noise = psum.tile([P, CHUNK], F32, name="noise%d" % c, tag="b%d" % c)
             nc.tensor.matmul_mx(
                 out=noise[:],
                 lhsT=codes[:, :N].bitcast(FP8X4),
@@ -212,7 +219,7 @@ def tile_picked_yddpm_relu_p_kernel(tc, x_words, x_scales, w1, w2, temb, lat, cs
             )
             return noise
 
-        pieces = [(0, 0, 2, "b7"), (0, 2, 2, "b0")] + [(c, 0, PACK, "b%d" % c) for c in range(1, CHUNKS)]
+        pieces = [(c, first, 2, "b%d" % (2 * c + first // 2)) for c in range(CHUNKS) for first in (0, 2)]
         accs = [first_product(*piece) for piece in pieces]
         for acc, (c, first, count, bank) in zip(accs, pieces):
             half, at = divmod(c * CHUNK, HALF)
@@ -226,7 +233,7 @@ def tile_picked_yddpm_relu_p_kernel(tc, x_words, x_scales, w1, w2, temb, lat, cs
 
         kept = held.tile([P, S], F32, name="kept")
         nc.gpsimd.tensor_tensor(kept[:], lat_sb, sig_factor, MULT)
-        removed = held.tile([P, S], F32, name="removed", tag="pre%d" % LAST)
+        removed = held.tile([P, S], F32, name="removed", tag="emb0", align_bytes=64)
         for c in range(CHUNKS):
             cols = slice(c * CHUNK, (c + 1) * CHUNK)
             nc.vector.tensor_tensor(removed[:, cols], second_product(c)[:], noise_factor[:, cols], MULT)

@@ -29,7 +29,6 @@ LANES = 16
 WINDOW = R + LANES
 SIG_ROW, NOISE_ROW = 126, 127
 SCALE_ROWS = 112
-W2_SPLIT = 32
 
 
 def tile_picked_yddpm_relu_p_kernel(tc, x_words, x_scales, w1, w2, temb, lat, csig, cnoise, offs, step, out):
@@ -45,7 +44,7 @@ def tile_picked_yddpm_relu_p_kernel(tc, x_words, x_scales, w1, w2, temb, lat, cs
         second = held.tile([P, R + 2 * CHUNKS], F32, name="second")
         third = held.tile([P, WINDOW], F32, name="third")
         coef = held.tile([P, WINDOW], F32, name="coef")
-        scale_table = shared.tile([P, T], U8, name="scale_table", offset=3072)
+        scale_table = held.tile([P, T], U8, name="scale_table")
         word_table = held.tile([P, T], I32, name="word_table")
         emb_g = [
             held.tile([P, PACK, HALF], F32, name="emb_g%d" % half, tag="emb%d" % half, align_bytes=64)
@@ -152,18 +151,8 @@ def tile_picked_yddpm_relu_p_kernel(tc, x_words, x_scales, w1, w2, temb, lat, cs
 
         staged = held.tile([P, PACK * (N + S)], BF16, name="staged", align_bytes=64)
         w2_cast = staged[:, : PACK * N]
-        nc.scalar.activation(
-            w2_cast[:, : PACK * W2_SPLIT].rearrange("p (a i j) -> p a j i", i=4, j=PACK),
-            w2_raw[:, :, :W2_SPLIT].rearrange("p j (a i) -> p a j i", i=4),
-            COPY,
-        )
         nc.gpsimd.tensor_scalar(
-            w2_cast[:, PACK * W2_SPLIT :].rearrange("p (m j) -> p m j", j=PACK),
-            w2_raw[:, :, W2_SPLIT:].rearrange("p j m -> p m j"),
-            1.0,
-            0.0,
-            MULT,
-            ADD,
+            w2_cast.rearrange("p (m j) -> p m j", j=PACK), w2_raw.rearrange("p j m -> p m j"), 1.0, 0.0, MULT, ADD
         )
 
         pre = [

@@ -29,6 +29,7 @@ LANES = 16
 WINDOW = R + LANES
 SIG_ROW, NOISE_ROW = 126, 127
 SCALE_ROWS = 112
+RELU_SPLIT = 96
 
 
 def tile_picked_yddpm_relu_p_kernel(tc, x_words, x_scales, w1, w2, temb, lat, csig, cnoise, offs, step, out):
@@ -181,10 +182,10 @@ def tile_picked_yddpm_relu_p_kernel(tc, x_words, x_scales, w1, w2, temb, lat, cs
                 )
             return acc
 
-        def relu_views(c):
+        def relu_views(c, first, count):
             return (
-                h_bf[c].rearrange("p (a i t) -> p a t i", i=4, t=PACK),
-                pre[c][:].rearrange("p t (a i) -> p a t i", i=4),
+                h_bf[c][:, PACK * first : PACK * (first + count)].rearrange("p (a i t) -> p a t i", i=4, t=PACK),
+                pre[c][:, :, first : first + count].rearrange("p t (a i) -> p a t i", i=4),
             )
 
         def quantise_staged(first, count):
@@ -215,8 +216,9 @@ def tile_picked_yddpm_relu_p_kernel(tc, x_words, x_scales, w1, w2, temb, lat, cs
             tiles = slice(first, first + count)
             nc.vector.tensor_tensor(pre[c][:, tiles, :], acc[:], emb_g[half][:, tiles, at : at + CHUNK], ADD)
             if first + count == PACK:
-                nc.scalar.activation(*relu_views(c), RELU)
+                nc.scalar.activation(*relu_views(c, 0, CHUNK if c < LAST else RELU_SPLIT), RELU)
         quantise_staged(0, N + CHUNK)
+        nc.vector.tensor_scalar_max(*relu_views(LAST, RELU_SPLIT, CHUNK - RELU_SPLIT), 0.0)
         for c in range(1, CHUNKS):
             quantise_staged(N + c * CHUNK, CHUNK)
 

@@ -29,7 +29,7 @@ LANES = 16
 WINDOW = R + LANES
 SIG_ROW, NOISE_ROW = 126, 127
 SCALE_ROWS = 112
-RELU_SPLIT = 96
+RELU_SPLIT = 80
 
 
 def tile_picked_yddpm_relu_p_kernel(tc, x_words, x_scales, w1, w2, temb, lat, csig, cnoise, offs, step, out):

from contextlib import ExitStack

import concourse.mybir as mybir
from concourse.masks import make_identity

K, T, S, H, N, R = 512, 2048, 512, 512, 128, 256
FLOPS = 2 * K * H * S + 2 * H * N * S

F32 = mybir.dt.float32
BF16 = mybir.dt.bfloat16
I32 = mybir.dt.int32
U32 = mybir.dt.uint32
U16 = mybir.dt.uint16
U8 = mybir.dt.uint8
FP8X4 = mybir.dt.float8_e4m3fn_x4
ADD = mybir.AluOpType.add
MULT = mybir.AluOpType.mult
SUBTRACT = mybir.AluOpType.subtract
COPY = mybir.ActivationFunctionType.Copy
RELU = mybir.ActivationFunctionType.Relu

P = 128
PACK = 4
CHUNK = 128
CHUNKS = S // CHUNK
HALF = S // 2
LAST = CHUNKS - 1
LANES = 16
WINDOW = R + LANES
SIG_ROW, NOISE_ROW = 126, 127
SCALE_ROWS = 112
RELU_SPLIT = 80


def tile_picked_yddpm_relu_p_kernel(tc, x_words, x_scales, w1, w2, temb, lat, csig, cnoise, offs, step, out):
    nc = tc.nc
    with ExitStack() as ctx:
        held = ctx.enter_context(tc.tile_pool(name="held", bufs=1))
        shared = ctx.enter_context(tc.tile_pool(name="shared", bufs=1))
        psum = ctx.enter_context(tc.psum_pool(name="psum", bufs=1))

        step_list = held.tile([P, S // LANES], U16, name="step_list")
        offs_list = held.tile([P, S // LANES], U16, name="offs_list")
        pair = held.tile([P, 2 * R], F32, name="pair")
        second = held.tile([P, R + 2 * CHUNKS], F32, name="second")
        third = held.tile([P, WINDOW], F32, name="third")
        coef = held.tile([P, WINDOW], F32, name="coef")
        scale_table = held.tile([P, T], U8, name="scale_table")
        word_table = held.tile([P, T], I32, name="word_table")
        emb_g = [
            held.tile([P, PACK, HALF], F32, name="emb_g%d" % half, tag="emb%d" % half, align_bytes=64)
            for half in range(2)
        ]
        w1_raw = held.tile([P, PACK, H], F32, name="w1_raw", tag="raw")
        x_sc = held.tile([P, S], U8, name="x_sc", align_bytes=64)
        ident = held.tile([P, P], F32, name="ident")

        nc.gpsimd.memset(coef[:, R:], 0.0)
        nc.gpsimd.memset(coef[:SIG_ROW, :R], 0.0)
        nc.gpsimd.memset(scale_table[:SCALE_ROWS, :].bitcast(I32), 0)
        nc.gpsimd.memset(x_sc[:].bitcast(I32), 0)
        make_identity(nc, ident[:])

        temb_rows = temb.rearrange("(p t) r -> p (t r)", t=PACK)
        nc.sync.dma_start(third[:, :R], temb_rows[:, 2 * R : 3 * R])
        nc.scalar.dma_start(coef[SIG_ROW : SIG_ROW + 1, :R], csig[0:1, :])
        nc.scalar.dma_start(coef[NOISE_ROW : NOISE_ROW + 1, :R], cnoise[0:1, :])
        nc.sync.dma_start(step_list[:], step)
        nc.sync.dma_start(offs_list[:], offs)
        nc.scalar.dma_start(scale_table[SCALE_ROWS:, :].bitcast(I32), x_scales[0].bitcast(I32))
        nc.scalar.activation(third[:, R:], coef[:, R:], COPY)
        nc.sync.dma_start(pair[:], temb_rows[:, : 2 * R])
        nc.sync.dma_start(w1_raw[:], w1.rearrange("(p j) c -> p j c", j=PACK))
        nc.sync.dma_start(word_table[:], x_words[0].rearrange("p n t -> p (n t)").bitcast(I32))

        def entries(lst, first, count):
            return lst[:, first // LANES : (first + count) // LANES]

        def plane_lookup(t, table, halves=(0, 1)):
            for half in halves:
                nc.scalar.activation(
                    emb_g[half][:, t, :], table[:].indirect(entries(step_list, half * HALF, HALF)), COPY
                )

        plane_lookup(2, third)
        plane_lookup(0, pair, (0,))
        nc.scalar.copy(second[:, :R], pair[:, R:])
        coef_g = held.tile([P, S], F32, name="coef_g")
        for half in range(2):
            nc.vector.tensor_copy(
                coef_g[:, half * HALF : (half + 1) * HALF], coef[:].indirect(entries(step_list, half * HALF, HALF))
            )
        picked_sc = held.tile([P, S], U8, name="picked_sc")
        nc.vector.tensor_copy(picked_sc[:], scale_table[:].indirect(offs_list[:]))
        for q in range(4):
            nc.sync.dma_start(
                x_sc[32 * q : 32 * q + 4, :].bitcast(I32),
                picked_sc[SCALE_ROWS + 4 * q : SCALE_ROWS + 4 * q + 4, :].bitcast(I32),
            )
        late = shared.tile([P, WINDOW], F32, name="late", offset=4096)
        nc.sync.dma_start(late[:, :R], temb_rows[:, LAST * R :])
        nc.vector.tensor_copy(emb_g[1][:, 0, :], pair[:].indirect(entries(step_list, HALF, HALF)))

        w1_bf = held.tile([P, PACK * H], BF16, name="w1_bf", align_bytes=64)
        for tiles in (slice(0, 2), slice(2, PACK)):
            nc.vector.tensor_copy(
                w1_bf[:].rearrange("p (t m j) -> p m j t", t=PACK, j=PACK)[:, :, :, tiles],
                w1_raw[:].rearrange("p j (m t) -> p m j t", t=PACK)[:, :, :, tiles],
            )
        w1_codes = held.tile([P, H], U32, name="w1_codes", align_bytes=64)
        w1_sc = held.tile([P, H], U8, name="w1_sc", align_bytes=64)
        for first in (0, H // 2):
            chans = slice(first, first + H // 2)
            nc.vector.quantize_mx(
                out=w1_codes[:, chans].bitcast(FP8X4),
                scales=w1_sc[:, chans],
                in_=w1_bf[:, PACK * first : PACK * (first + H // 2)],
            )

        tail_raw = held.tile([P, PACK * N + S], F32, name="tail_raw", tag="raw")
        w2_raw = tail_raw[:, : PACK * N].rearrange("p (j m) -> p j m", j=PACK)
        lat_sb = tail_raw[:, PACK * N :]
        nc.sync.dma_start(w2_raw, w2.rearrange("(p j) m -> p j m", j=PACK))
        nc.sync.dma_start(lat_sb, lat)

        x_codes = held.tile([P, S], U32, name="x_codes", align_bytes=64)
        for first, count in ((0, CHUNK), (CHUNK, CHUNK), (HALF, HALF)):
            nc.vector.tensor_copy(
                x_codes[:, first : first + count],
                word_table[:].bitcast(U32).indirect(entries(offs_list, first, count)),
            )

        coef_t = psum.tile([P, CHUNKS, P], F32, name="coef_t", tag="b4")
        for c in range(CHUNKS):
            nc.tensor.transpose(coef_t[:, c, :], coef_g[:, c * CHUNK : (c + 1) * CHUNK], ident[:])
        coef_col = second[:, R:].rearrange("p (c s) -> p c s", s=2)
        nc.scalar.copy(coef_col, coef_t[:, :, SIG_ROW:])
        plane_lookup(1, second)
        factor = held.tile([P, 2, S], F32, name="factor")
        for s in range(2):
            factor_ps = psum.tile([P, S], F32, name="factor_ps%d" % s, tag="b%d" % (5 + s))
            for c in range(CHUNKS):
                nc.tensor.transpose(
                    factor_ps[:, c * CHUNK : (c + 1) * CHUNK],
                    coef_col[:, c, s : s + 1].to_broadcast([P, P]),
                    ident[:],
                )
            nc.scalar.copy(factor[:, s, :], factor_ps[:])
        sig_factor, noise_factor = factor[:, 0, :], factor[:, 1, :]
        nc.scalar.copy(late[:, R:], factor_ps[:, :LANES])
        plane_lookup(LAST, late)

        staged = held.tile([P, PACK * (N + S)], BF16, name="staged", align_bytes=64)
        w2_cast = staged[:, : PACK * N]
        nc.gpsimd.tensor_scalar(
            w2_cast.rearrange("p (m j) -> p m j", j=PACK), w2_raw.rearrange("p j m -> p m j"), 1.0, 0.0, MULT, ADD
        )

        pre = [
            held.tile([P, PACK, CHUNK], F32, name="pre0"),
            shared.tile([P, PACK, CHUNK], F32, name="pre1", offset=2112),
            shared.tile([P, PACK, CHUNK], F32, name="pre2", offset=4160),
            held.tile([P, PACK, CHUNK], F32, name="pre3", tag="emb0", align_bytes=64),
        ]
        h_bf = [staged[:, PACK * (N + c * CHUNK) : PACK * (N + (c + 1) * CHUNK)] for c in range(CHUNKS)]
        codes = held.tile([P, N + S], U32, name="codes", tag="codes", align_bytes=64)
        scales = held.tile([P, N + S], U8, name="code_scales", align_bytes=64)

        def first_product(c, first, count, bank):
            cols = slice(c * CHUNK, (c + 1) * CHUNK)
            acc = psum.tile([P, count, CHUNK], F32, name="acc%d_%d" % (c, first), tag=bank)
            for t in range(first, first + count):
                chans = slice(t * P, (t + 1) * P)
                nc.tensor.matmul_mx(
                    out=acc[:, t - first, :],
                    lhsT=w1_codes[:, chans].bitcast(FP8X4),
                    lhsT_scale=w1_sc[:, chans],
                    rhs=x_codes[:, cols].bitcast(FP8X4),
                    rhs_scale=x_sc[:, cols],
                    start=True,
                    stop=True,
                )
            return acc

        def relu_views(c, first, count):
            return (
                h_bf[c][:, PACK * first : PACK * (first + count)].rearrange("p (a i t) -> p a t i", i=4, t=PACK),
                pre[c][:, :, first : first + count].rearrange("p t (a i) -> p a t i", i=4),
            )

        def quantise_staged(first, count):
            nc.vector.quantize_mx(
                out=codes[:, first : first + count].bitcast(FP8X4),
                scales=scales[:, first : first + count],
                in_=staged[:, PACK * first : PACK * (first + count)],
            )

        def second_product(c):
            cols = slice(N + c * CHUNK, N + (c + 1) * CHUNK)
            noise = psum.tile([P, CHUNK], F32, name="noise%d" % c, tag="b%d" % c)
            nc.tensor.matmul_mx(
                out=noise[:],
                lhsT=codes[:, :N].bitcast(FP8X4),
                lhsT_scale=scales[:, :N],
                rhs=codes[:, cols].bitcast(FP8X4),
                rhs_scale=scales[:, cols],
                start=True,
                stop=True,
            )
            return noise

        pieces = [(c, first, 2, "b%d" % (2 * c + first // 2)) for c in range(CHUNKS) for first in (0, 2)]
        accs = [first_product(*piece) for piece in pieces]
        for acc, (c, first, count, bank) in zip(accs, pieces):
            half, at = divmod(c * CHUNK, HALF)
            tiles = slice(first, first + count)
            nc.vector.tensor_tensor(pre[c][:, tiles, :], acc[:], emb_g[half][:, tiles, at : at + CHUNK], ADD)
            if first + count == PACK:
                nc.scalar.activation(*relu_views(c, 0, CHUNK if c < LAST else RELU_SPLIT), RELU)
        quantise_staged(0, N + CHUNK)
        nc.vector.tensor_scalar_max(*relu_views(LAST, RELU_SPLIT, CHUNK - RELU_SPLIT), 0.0)
        for c in range(1, CHUNKS):
            quantise_staged(N + c * CHUNK, CHUNK)

        kept = held.tile([P, S], F32, name="kept")
        nc.gpsimd.tensor_tensor(kept[:], lat_sb, sig_factor, MULT)
        removed = held.tile([P, S], F32, name="removed", tag="emb0", align_bytes=64)
        for c in range(CHUNKS):
            cols = slice(c * CHUNK, (c + 1) * CHUNK)
            nc.vector.tensor_tensor(removed[:, cols], second_product(c)[:], noise_factor[:, cols], MULT)
        early = held.tile([P, CHUNK], F32, name="early")
        nc.gpsimd.tensor_tensor(early[:], kept[:, :CHUNK], removed[:, :CHUNK], SUBTRACT)
        nc.sync.dma_start(out[:, :CHUNK], early[:])
        result = held.tile([P, S], F32, name="result", tag="codes", align_bytes=64)
        for cols in (slice(CHUNK, LAST * CHUNK), slice(LAST * CHUNK, S)):
            nc.vector.tensor_tensor(result[:, cols], kept[:, cols], removed[:, cols], SUBTRACT)
            nc.sync.dma_start(out[:, cols], result[:, cols])
